import numpy as np
import ml_dtypes


def mxq(x, axis, fmt="e4m3"):
    dtype, down = {"e4m3": (ml_dtypes.float8_e4m3fn, 7), "e5m2": (ml_dtypes.float8_e5m2, 14)}[fmt]
    v = np.moveaxis(np.asarray(x, np.float32).astype(ml_dtypes.bfloat16).astype(np.float64), axis, -1)
    blocks = v.reshape(v.shape[:-1] + (-1, 32))
    amax = np.abs(blocks).max(-1, keepdims=True)
    byte = np.maximum(np.where(amax > 0, np.frexp(amax)[1] - 1 + 127, 0) - down, 1)
    scale = np.exp2(byte - 127.0)
    codes = (blocks / scale).astype(np.float32).astype(dtype).astype(np.float64)
    return np.moveaxis((codes * scale).reshape(v.shape), -1, axis)


WIDE = False


def mx_kscale(k):
    if not WIDE:
        return np.ones(k)
    levels = np.array([10, -10, 5, -5, 0])
    if k % 512:
        return np.exp2(np.random.permutation(np.resize(levels, k // 32))).repeat(32)
    a = np.empty((k // 512, 16))
    for p in range(k // 512):
        a[p, :8] = np.random.permutation(np.resize(levels, 8))
        for g in range(8):
            far = levels[np.abs(levels - a[p, g]) >= 10]
            a[p, g + 8] = far[np.random.randint(len(far))]
    return np.exp2(a.ravel()).repeat(32)


def f64(x):
    return np.asarray(x).astype(np.float64)


def striped(idx):
    return np.tile(idx.reshape(-1, 16).T, (8, 1)).astype(np.uint16)


def unstriped(offs):
    return offs[:16].T.reshape(-1).astype(np.int64)


E2M1 = np.array([0.0, 0.5, 1.0, 1.5, 2.0, 3.0, 4.0, 6.0, -0.0, -0.5, -1.0, -1.5, -2.0, -3.0, -4.0, -6.0])


def pack_weight(w, fmt):
    k, n = w.shape
    w = f64(np.asarray(w, np.float32).astype(ml_dtypes.bfloat16)).reshape(k // 32, 32, n)
    amax = np.abs(w).max(1)
    if fmt == "e4m3":
        byte = np.frexp(amax)[1] - 1 + 127 - 7
    else:
        mant, ex = np.frexp(amax / 6.0)
        byte = np.where(mant > 0.5, ex, ex - 1) + 127
    byte = np.clip(np.where(amax > 0, byte, 1), 1, 254)
    scaled = (w * np.exp2(127.0 - byte)[:, None, :]).reshape(k, n).astype(np.float32)
    by_word = np.ascontiguousarray(scaled.reshape(k // 512, 128, 4, n).transpose(0, 1, 3, 2))
    if fmt == "e4m3":
        words = by_word.astype(ml_dtypes.float8_e4m3fn).view(np.uint8)
    else:
        c = by_word.astype(ml_dtypes.float4_e2m1fn).view(np.uint8) & 0xF
        words = (c[..., 0::2] | (c[..., 1::2] << 4)).reshape(k // 512, 128, 2 * n)
    return np.ascontiguousarray(words), np.ascontiguousarray(byte.astype(np.uint8).reshape(k // 512, 16, n))


def unpack_weight(words, scales, fmt):
    g, _, n = scales.shape
    words = np.ascontiguousarray(words).reshape(g, 128, n, -1)
    if fmt == "e4m3":
        vals = words.view(ml_dtypes.float8_e4m3fn).astype(np.float64)
    else:
        nib = np.empty((g, 128, n, 4), np.uint8)
        nib[..., 0::2] = words & 0xF
        nib[..., 1::2] = words >> 4
        vals = E2M1[nib]
    vals = vals * np.repeat(np.exp2(scales.astype(np.float64) - 127.0), 8, axis=1)[..., None]
    return vals.transpose(0, 1, 3, 2).reshape(g * 512, n)


def gelu(v):
    return 0.5 * v * (1.0 + np.tanh(np.sqrt(2.0 / np.pi) * (v + 0.044715 * v**3)))


def striped8(idx):
    return np.concatenate([v.reshape(-1, 16).T for v in idx]).astype(np.uint16)


def unstriped8(offs):
    return np.stack([offs[16 * g:16 * g + 16].T.reshape(-1) for g in range(8)]).astype(np.int64)


def heads(h, wgt, idx8):
    r = np.arange(h.shape[0])
    return wgt[r // 4 % 128] * h[r[:, None], idx8[r % 512 // 64]]


def put_heads(h, wgs, idx8, t2):
    r = np.arange(h.shape[0])
    page = np.zeros((h.shape[0], t2))
    page[r[:, None], idx8[r % 512 // 64]] = wgs[r // 4 % 128] * h
    return page


K, T, S, H, P, N, T2 = 1024, 2048, 1024, 1024, 512, 512, 1024


def setup_inputs():
    n = np.random.standard_normal
    s, u = mx_kscale(K)[:, None], mx_kscale(H)[:, None]
    d = {}
    d["tab_words"], d["tab_scales"] = pack_weight(n((K, T)) * s, "e4m3")
    d["offs"] = striped(np.random.permutation(T)[:S])
    d["w1"] = (n((K, H)) / s / K**0.5).astype(np.float32)
    d["w2_words"], d["w2_scales"] = pack_weight(n((K, H)) / s / K**0.5, "e2m1")
    d["ga"] = (0.8 * np.exp(0.4 * n(H))).astype(np.float32)
    d["offs2"] = striped8(np.stack([np.random.permutation(S)[:P] for _ in range(8)]))
    d["wgt"] = np.repeat(np.random.uniform(0.5, 2.0, (8, P)), 16, axis=0).astype(np.float32)
    d["sv"] = (0.7 * np.exp(0.3 * n(H))).astype(np.float32)
    d["gu"] = (np.exp(0.4 * n(H)) * u[:, 0]).astype(np.float32)
    d["w3"] = (n((H, N)) / u / H**0.5).astype(np.float32)
    d["w4_words"], d["w4_scales"] = pack_weight(n((H, N)) / u / H**0.5, "e4m3")
    d["offs3"] = striped8(np.stack([np.random.permutation(T2)[:P] for _ in range(8)]))
    d["wgo"] = np.repeat(np.random.uniform(0.5, 2.0, (8, P)), 16, axis=0).astype(np.float32)
    return d


def reference(tab_words, tab_scales, offs, w1, w2_words, w2_scales, ga, offs2, wgt, sv, gu,
              w3, w4_words, w4_scales, offs3, wgo):
    v = unpack_weight(tab_words, tab_scales, "e4m3")[:, unstriped(offs)]
    b1 = mxq(f64(w1), 0, "e4m3").T @ v
    b2 = unpack_weight(w2_words, w2_scales, "e2m1").T @ v
    h = b1 - f64(ga)[:, None] * np.abs(b2)
    x = heads(h, f64(wgt), unstriped8(offs2))
    x = np.tanh(x * f64(sv)[:, None]) * f64(gu)[:, None]
    xq = mxq(x, 0, "e4m3")
    y3 = mxq(f64(w3), 0, "e4m3").T @ xq
    y4 = unpack_weight(w4_words, w4_scales, "e4m3").T @ xq
    y = np.maximum(y3, y4)
    return put_heads(y, f64(wgo), unstriped8(offs3), T2)

@@ -1,0 +1,314 @@
+from contextlib import ExitStack
+
+import concourse.mybir as mybir
+
+K, T, S, H, M, N, SLOTS = 1024, 2048, 1024, 1024, 512, 512, 1024
+FLOPS = 2 * (2 * K * H * S) + 2 * (2 * H * N * M)
+
+F32 = mybir.dt.float32
+BF16 = mybir.dt.bfloat16
+I32 = mybir.dt.int32
+U32 = mybir.dt.uint32
+U16 = mybir.dt.uint16
+U8 = mybir.dt.uint8
+FP8X4 = mybir.dt.float8_e4m3fn_x4
+FP4X4 = mybir.dt.float4_e2m1fn_x4
+ACT = mybir.ActivationFunctionType
+ALU = mybir.AluOpType
+
+P = 128
+PACK = 4
+KP = P * PACK
+BANK = 512
+HALF = M // 2
+PER_COL = 16
+
+
+def tile_list_stigma_purity_scores_kernel(
+    tc, tab_words, tab_scales, offs, w1, w2_words, w2_scales, ga, offs2, wgt, sv, gu,
+    w3, w4_words, w4_scales, offs3, wgo, out
+):
+    nc = tc.nc
+    with ExitStack() as ctx:
+        keep = ctx.enter_context(tc.tile_pool(name="keep", bufs=1))
+        ring = ctx.enter_context(tc.tile_pool(name="ring", bufs=4))
+        psum = ctx.enter_context(tc.psum_pool(name="psum", bufs=4))
+
+        def held(shape, dtype, name):
+            return keep.tile(shape, dtype, name=name, tag=name, align_bytes=64)
+
+        tab_sc = held([P, T], U8, "tab_sc")
+        w_sc = held([P, KP], U8, "w_sc")
+        v_sc = held([P, 2, S], U8, "v_sc")
+        w2p_sc = held([P, 4, KP], U8, "w2p_sc")
+        w4p_sc = held([P, 2, N], U8, "w4p_sc")
+        nc.vector.memset(w_sc[:].bitcast(I32)[96:128, :], 0)
+        nc.vector.memset(tab_sc[:].bitcast(I32)[32:64, :], 0)
+        nc.vector.memset(tab_sc[:].bitcast(I32)[64:128, :], 0)
+        for plane in (w2p_sc, v_sc, w4p_sc):
+            nc.vector.memset(plane[:].bitcast(I32), 0)
+
+        warm_in = held([P, 1], F32, "warm_in")
+        warm_out = held([P, 1], F32, "warm_out")
+        nc.gpsimd.memset(warm_in[:], 0.0)
+        nc.scalar.activation(out=warm_out[:], in_=warm_in[:], func=ACT.Tanh)
+
+        list1 = keep.tile([P, S // PER_COL], U16, name="list1")
+        nc.sync.dma_start(list1[:], offs)
+        nc.sync.dma_start(out=tab_sc[:].bitcast(I32)[0:32, :],
+                          in_=tab_scales.rearrange("a q t -> q a t").bitcast(I32))
+        nc.sync.dma_start(out=w_sc[:].bitcast(I32)[0:64, :],
+                          in_=w2_scales.rearrange("a q (b c) -> (q b) a c", b=2).bitcast(I32))
+        nc.sync.dma_start(out=w_sc[:].bitcast(I32)[64:96, :],
+                          in_=w4_scales.rearrange("a q c -> q a c").bitcast(I32))
+        tab_w = []
+        for a in range(2):
+            tw = held([P, T], I32, "tab_w%d" % a)
+            nc.sync.dma_start(out=tw[:], in_=tab_words[a].rearrange("p t i -> p (t i)").bitcast(I32))
+            tab_w.append(tw)
+        w2_w = held([P, 2, H // 2], I32, "w2_w")
+        nc.sync.dma_start(out=w2_w[:], in_=w2_words.rearrange("a p c -> p a c").bitcast(I32))
+
+        def load_rows(w, a, b):
+            raw = ring.tile([P, PACK, KP], F32, name="raw", align_bytes=64)
+            src = w[a * KP:(a + 1) * KP, b * KP:(b + 1) * KP]
+            nc.sync.dma_start(out=raw[:], in_=src.rearrange("(p j) c -> p j c", j=PACK))
+            return raw
+
+        def load_vec(vec, name):
+            v = held([P, 2, PACK], F32, name)
+            nc.sync.dma_start(out=v[:], in_=vec.rearrange("(b p i) -> p b i", b=2, i=PACK))
+            return v
+
+        w1_raw = {}
+        w1_raw[0, 0] = load_rows(w1, 0, 0)
+        w1_raw[1, 0] = load_rows(w1, 1, 0)
+        ga_t = load_vec(ga, "ga_t")
+        list2 = keep.tile([P, M // PER_COL], U16, name="list2")
+        nc.sync.dma_start(list2[:], offs2)
+        wgt_t = held([P, M], F32, "wgt_t")
+        nc.sync.dma_start(out=wgt_t[:], in_=wgt)
+        sv_t = load_vec(sv, "sv_t")
+        gu_t = load_vec(gu, "gu_t")
+        w1_raw[0, 1] = load_rows(w1, 0, 1)
+        w1_raw[1, 1] = load_rows(w1, 1, 1)
+        w3_raw = [load_rows(w3, a, 0) for a in range(2)]
+        w4_w = held([P, 2, N], I32, "w4_w")
+        nc.sync.dma_start(out=w4_w[:], in_=w4_words.rearrange("a p c i -> p a (c i)").bitcast(I32))
+        list3 = keep.tile([P, M // PER_COL], U16, name="list3")
+        nc.sync.dma_start(list3[:], offs3)
+        wgo_t = held([P, M], F32, "wgo_t")
+        nc.sync.dma_start(out=wgo_t[:], in_=wgo)
+
+        def place_rows(queue, plane, rows, first, count):
+            for q in range(4):
+                queue.dma_start(out=plane[:].bitcast(I32)[32 * q:32 * q + 4],
+                                in_=rows[:].bitcast(I32)[first + count * q:first + count * (q + 1), :])
+
+        dealt_sc = held([P, KP], U8, "dealt_sc")
+        nc.vector.tensor_copy(out=dealt_sc[:].rearrange("p (t m) -> p t m", t=PACK),
+                              in_=w_sc[:].rearrange("p (m t) -> p t m", t=PACK))
+        place_rows(nc.gpsimd, w2p_sc, dealt_sc, 0, 16)
+        picked_sc = held([P, S], U8, "picked_sc")
+        nc.vector.tensor_copy(out=picked_sc[:], in_=tab_sc[:].indirect(list1[:]))
+        place_rows(nc.gpsimd, v_sc, picked_sc, 0, 8)
+        v_w = {}
+
+        def gather_words(a, c):
+            g = held([P, BANK], U32, "v_w%d%d" % (a, c))
+            cols = BANK // PER_COL
+            nc.vector.tensor_copy(out=g[:], in_=tab_w[a][:].bitcast(U32).indirect(list1[:, c * cols:(c + 1) * cols]))
+            v_w[a, c] = g
+
+        gather_words(0, 0)
+        gather_words(0, 1)
+        gather_words(1, 0)
+        gather_words(1, 1)
+
+        w2p = []
+        for b in range(2):
+            wp = held([P, 2, 2 * KP], U8, "w2p%d" % b)
+            src = w2_w[:].bitcast(U16)[:, :, b * KP:(b + 1) * KP]
+            nc.vector.tensor_copy(out=wp[:].bitcast(U16).rearrange("p a (t m) -> p a t m", t=PACK),
+                                  in_=src.rearrange("p a (m t) -> p a t m", t=PACK))
+            w2p.append(wp)
+
+        nga = held([P, 2, PACK], F32, "nga")
+        nc.vector.tensor_scalar(out=nga[:], in0=ga_t[:], scalar1=-1.0, scalar2=None, op0=ALU.mult)
+
+        def cast(raw, vector_cols):
+            grouped = ring.tile([P, KP * PACK], BF16, name="grouped", align_bytes=64, bufs=3)
+            dst = grouped[:].rearrange("p (t m j) -> p m j t", t=PACK, j=PACK)
+            src = raw[:].rearrange("p j (m t) -> p m j t", t=PACK)
+            if vector_cols > 0:
+                nc.vector.tensor_copy(out=dst[:, :vector_cols], in_=src[:, :vector_cols])
+            if vector_cols < P:
+                nc.scalar.copy(out=dst[:, vector_cols:], in_=src[:, vector_cols:])
+            return grouped
+
+        def quantize(grouped, width, name):
+            codes = held([P, width], U32, name + "_w")
+            scales = held([P, width], U8, name + "_s")
+            nc.vector.quantize_mx(out=codes[:].bitcast(FP8X4), scales=scales[:], in_=grouped[:])
+            return codes, scales
+
+        h = {}
+
+        def foreign(b, i):
+            ht = held([P, S], F32, "h%d%d" % (b, i))
+            for c in range(2):
+                cols = slice(c * BANK, (c + 1) * BANK)
+                acc = psum.tile([P, BANK], F32, name="acc_s")
+                for a in range(2):
+                    nc.tensor.matmul_mx(
+                        out=acc[:],
+                        lhsT=w2p[b][:, a, 2 * P * i:2 * P * (i + 1)].bitcast(FP4X4),
+                        lhsT_scale=w2p_sc[:, 2 * b + a, P * i:P * (i + 1)],
+                        rhs=v_w[a, c][:].bitcast(FP8X4), rhs_scale=v_sc[:, a, cols],
+                        start=(a == 0), stop=(a == 1))
+                nc.scalar.activation(out=ht[:, cols], in_=acc[:], func=ACT.Abs)
+            h[b, i] = ht
+
+        w1q = {}
+
+        def stigma(b, i):
+            ht = h[b, i]
+            for c in range(2):
+                cols = slice(c * BANK, (c + 1) * BANK)
+                acc = psum.tile([P, BANK], F32, name="acc_v")
+                for a in range(2):
+                    codes, scales = w1q[a, b]
+                    nc.tensor.matmul_mx(
+                        out=acc[:],
+                        lhsT=codes[:, P * i:P * (i + 1)].bitcast(FP8X4),
+                        lhsT_scale=scales[:, P * i:P * (i + 1)],
+                        rhs=v_w[a, c][:].bitcast(FP8X4), rhs_scale=v_sc[:, a, cols],
+                        start=(a == 0), stop=(a == 1))
+                nc.vector.scalar_tensor_tensor(out=ht[:, cols], in0=ht[:, cols], scalar=nga[:, b, i:i + 1],
+                                               in1=acc[:], op0=ALU.mult, op1=ALU.add)
+
+        planes = {}
+
+        def pick(b, i, u):
+            if i == 0:
+                planes[b, u] = ring.tile([P, PACK, HALF], BF16, name="xs", align_bytes=64)
+            cols = HALF // PER_COL
+            z = ring.tile([P, HALF], F32, name="z", align_bytes=64, bufs=8)
+            nc.vector.tensor_tensor(out=z[:], in0=h[b, i][:].indirect(list2[:, u * cols:(u + 1) * cols]),
+                                    in1=wgt_t[:, u * HALF:(u + 1) * HALF], op=ALU.mult)
+            th = ring.tile([P, HALF], F32, name="th", align_bytes=64)
+            nc.scalar.activation(out=th[:], in_=z[:], func=ACT.Tanh, scale=sv_t[:, b, i:i + 1])
+            nc.scalar.activation(out=planes[b, u][:, i, :], in_=th[:], func=ACT.Copy, scale=gu_t[:, b, i:i + 1])
+
+        xq = {}
+
+        def features(b, u):
+            xi = ring.tile([P, HALF * PACK], BF16, name="xi", align_bytes=64, bufs=2)
+            nc.vector.tensor_copy(out=xi[:].rearrange("p (c e t) -> p c t e", e=4, t=PACK),
+                                  in_=planes[b, u][:].rearrange("p t (c e) -> p c t e", e=4))
+            xq[b, u] = quantize(xi, HALF, "x%d%d" % (b, u))
+
+        g00 = cast(w1_raw[0, 0], 0)
+        g10 = cast(w1_raw[1, 0], P // 2)
+        for i in range(PACK):
+            foreign(0, i)
+        w1q[0, 0] = quantize(g00, KP, "w1q00")
+        w1q[1, 0] = quantize(g10, KP, "w1q10")
+
+        g01 = cast(w1_raw[0, 1], 0)
+        stigma(0, 0)
+        pick(0, 0, 0)
+        g11 = cast(w1_raw[1, 1], 0)
+        stigma(0, 1)
+        w1q[0, 1] = quantize(g01, KP, "w1q01")
+        pick(0, 1, 0)
+        foreign(1, 0)
+        stigma(0, 2)
+        pick(0, 2, 0)
+        foreign(1, 1)
+        stigma(0, 3)
+        w1q[1, 1] = quantize(g11, KP, "w1q11")
+        pick(0, 3, 0)
+        foreign(1, 2)
+        stigma(1, 0)
+        features(0, 0)
+        pick(1, 0, 0)
+        foreign(1, 3)
+        g3 = [cast(w3_raw[0], 0)]
+        stigma(1, 1)
+        pick(1, 1, 0)
+        g3.append(cast(w3_raw[1], 0))
+        stigma(1, 2)
+        pick(1, 2, 0)
+        stigma(1, 3)
+        pick(1, 3, 0)
+        w3q = [quantize(g3[a], N, "w3q%d" % a) for a in range(2)]
+
+        place_rows(nc.sync, w4p_sc, dealt_sc, 64, 8)
+        w4p = held([P, 2, N], I32, "w4p")
+        nc.vector.tensor_copy(out=w4p[:].rearrange("p a (t m) -> p a m t", t=PACK),
+                              in_=w4_w[:].rearrange("p a (m t) -> p a m t", t=PACK))
+
+        pages = [keep.tile([P, SLOTS], F32, name="page%d" % i, tag=tag, align_bytes=64)
+                 for i, tag in enumerate(("page0", "tab_w0", "tab_w1", "w2_w"))]
+        for page in pages:
+            nc.vector.memset(page[:], 0.0)
+
+        ys = {}
+
+        def scores(u, pair):
+            acc3 = psum.tile([P, BANK], F32, name="acc_s")
+            acc4 = psum.tile([P, BANK], F32, name="acc_v")
+            for e in range(2):
+                i = 2 * pair + e
+                cols = slice(e * HALF, (e + 1) * HALF)
+                for a in range(2):
+                    nc.tensor.matmul_mx(
+                        out=acc3[:, cols],
+                        lhsT=w3q[a][0][:, P * i:P * (i + 1)].bitcast(FP8X4),
+                        lhsT_scale=w3q[a][1][:, P * i:P * (i + 1)],
+                        rhs=xq[a, u][0][:].bitcast(FP8X4), rhs_scale=xq[a, u][1][:],
+                        start=(a == 0), stop=(a == 1))
+            for e in range(2):
+                i = 2 * pair + e
+                cols = slice(e * HALF, (e + 1) * HALF)
+                for a in range(2):
+                    nc.tensor.matmul_mx(
+                        out=acc4[:, cols],
+                        lhsT=w4p[:, a, P * i:P * (i + 1)].bitcast(FP8X4),
+                        lhsT_scale=w4p_sc[:, a, P * i:P * (i + 1)],
+                        rhs=xq[a, u][0][:].bitcast(FP8X4), rhs_scale=xq[a, u][1][:],
+                        start=(a == 0), stop=(a == 1))
+            y3 = ring.tile([P, BANK], F32, name="y3", align_bytes=64, bufs=2)
+            nc.scalar.copy(out=y3[:], in_=acc3[:])
+            y = ring.tile([P, BANK], F32, name="y", align_bytes=64)
+            nc.vector.tensor_tensor(out=y[:], in0=acc4[:], in1=y3[:], op=ALU.max)
+            ys[u, pair] = y
+
+        rows_out = out.rearrange("(p i) s -> p i s", i=PACK)
+
+        def file_scores(u, i):
+            cols = HALF // PER_COL
+            y = ys[u, i // 2][:, (i % 2) * HALF:(i % 2 + 1) * HALF]
+            nc.vector.tensor_tensor(out=pages[i][:].indirect(list3[:, u * cols:(u + 1) * cols]), in0=y,
+                                    in1=wgo_t[:, u * HALF:(u + 1) * HALF], op=ALU.mult)
+            if u == 1:
+                nc.sync.dma_start(out=rows_out[:, i, :], in_=pages[i][:])
+
+        for i in range(PACK):
+            pick(0, i, 1)
+        features(1, 0)
+        for i in range(PACK):
+            pick(1, i, 1)
+        features(0, 1)
+        scores(0, 0)
+        scores(0, 1)
+        file_scores(0, 0)
+        features(1, 1)
+        file_scores(0, 1)
+        file_scores(0, 2)
+        scores(1, 0)
+        file_scores(0, 3)
+        scores(1, 1)
+        for i in range(PACK):
+            file_scores(1, i)

@@ -32,47 +32,41 @@ def tile_list_stigma_purity_scores_kernel(
     with ExitStack() as ctx:
         keep = ctx.enter_context(tc.tile_pool(name="keep", bufs=1))
         ring = ctx.enter_context(tc.tile_pool(name="ring", bufs=4))
+        arena = ctx.enter_context(tc.tile_pool(name="arena", bufs=1))
         psum = ctx.enter_context(tc.psum_pool(name="psum", bufs=4))
 
         def held(shape, dtype, name):
             return keep.tile(shape, dtype, name=name, tag=name, align_bytes=64)
 
         tab_sc = held([P, T], U8, "tab_sc")
-        w_sc = held([P, KP], U8, "w_sc")
-        v_sc = held([P, 2, S], U8, "v_sc")
-        w2p_sc = held([P, 4, KP], U8, "w2p_sc")
-        w4p_sc = held([P, 2, N], U8, "w4p_sc")
-        nc.vector.memset(w_sc[:].bitcast(I32)[96:128, :], 0)
-        nc.vector.memset(tab_sc[:].bitcast(I32)[32:64, :], 0)
-        nc.vector.memset(tab_sc[:].bitcast(I32)[64:128, :], 0)
-        for plane in (w2p_sc, v_sc, w4p_sc):
-            nc.vector.memset(plane[:].bitcast(I32), 0)
+        w2_sc = held([P, 2, H], U8, "w2_sc")
+        w4_sc = held([P, N], U8, "w4_sc")
+        v_sc1 = held([P, S], U8, "v_sc1")
+        nc.gpsimd.memset(tab_sc[:].bitcast(I32), 0)
+        nc.vector.memset(w2_sc[:].bitcast(I32), 0)
+        nc.vector.memset(v_sc1[:].bitcast(I32)[96:128, :], 0)
+        nc.vector.memset(w4_sc[:].bitcast(I32), 0)
 
         warm_in = held([P, 1], F32, "warm_in")
         warm_out = held([P, 1], F32, "warm_out")
-        nc.gpsimd.memset(warm_in[:], 0.0)
+        nc.vector.memset(warm_in[:], 0.0)
         nc.scalar.activation(out=warm_out[:], in_=warm_in[:], func=ACT.Tanh)
 
-        list1 = keep.tile([P, S // PER_COL], U16, name="list1")
-        nc.sync.dma_start(list1[:], offs)
-        nc.sync.dma_start(out=tab_sc[:].bitcast(I32)[0:32, :],
-                          in_=tab_scales.rearrange("a q t -> q a t").bitcast(I32))
-        nc.sync.dma_start(out=w_sc[:].bitcast(I32)[0:64, :],
-                          in_=w2_scales.rearrange("a q (b c) -> (q b) a c", b=2).bitcast(I32))
-        nc.sync.dma_start(out=w_sc[:].bitcast(I32)[64:96, :],
-                          in_=w4_scales.rearrange("a q c -> q a c").bitcast(I32))
-        tab_w = []
-        for a in range(2):
-            tw = held([P, T], I32, "tab_w%d" % a)
-            nc.sync.dma_start(out=tw[:], in_=tab_words[a].rearrange("p t i -> p (t i)").bitcast(I32))
-            tab_w.append(tw)
-        w2_w = held([P, 2, H // 2], I32, "w2_w")
-        nc.sync.dma_start(out=w2_w[:], in_=w2_words.rearrange("a p c -> p a c").bitcast(I32))
+        def load_scale_rows(queue, dst, src):
+            rows = src.rearrange("a (q r) c -> r q a c", r=4)
+            for r in range(4):
+                queue.dma_start(out=dst[:].bitcast(I32)[r:P:16, :], in_=rows[r].bitcast(I32))
 
-        def load_rows(w, a, b):
-            raw = ring.tile([P, PACK, KP], F32, name="raw", align_bytes=64)
-            src = w[a * KP:(a + 1) * KP, b * KP:(b + 1) * KP]
-            nc.sync.dma_start(out=raw[:], in_=src.rearrange("(p j) c -> p j c", j=PACK))
+        raws = []
+
+        def load_rows(w, a, b, place, pieces=1):
+            raw = arena.tile([P, PACK, KP], F32, name="raw%d" % len(raws), align_bytes=64, offset=place * 8192)
+            raws.append(raw)
+            src = w[a * KP:(a + 1) * KP, b * KP:(b + 1) * KP].rearrange("(p j) c -> p j c", j=PACK)
+            width = KP // pieces
+            for n in range(pieces):
+                cols = slice(n * width, (n + 1) * width)
+                nc.sync.dma_start(out=raw[:, :, cols], in_=src[:, :, cols])
             return raw
 
         def load_vec(vec, name):
@@ -80,38 +74,49 @@ def tile_list_stigma_purity_scores_kernel(
             nc.sync.dma_start(out=v[:], in_=vec.rearrange("(b p i) -> p b i", b=2, i=PACK))
             return v
 
-        w1_raw = {}
-        w1_raw[0, 0] = load_rows(w1, 0, 0)
-        w1_raw[1, 0] = load_rows(w1, 1, 0)
+        def load_table(a):
+            tw = held([P, T], I32, "tab_w%d" % a)
+            nc.sync.dma_start(out=tw[:], in_=tab_words[a].rearrange("p t i -> p (t i)").bitcast(I32))
+            return tw
+
+        list1 = keep.tile([P, S // PER_COL], U16, name="list1")
+        nc.sync.dma_start(list1[:], offs)
         ga_t = load_vec(ga, "ga_t")
         list2 = keep.tile([P, M // PER_COL], U16, name="list2")
         nc.sync.dma_start(list2[:], offs2)
+        load_scale_rows(nc.sync, tab_sc, tab_scales)
+        tab_w = [load_table(0)]
+        for q in range(4):
+            nc.sync.dma_start(out=w2_sc[:].bitcast(I32)[32 * q:32 * q + 4],
+                              in_=w2_scales[:, 4 * q:4 * q + 4, :].rearrange("a r c -> r a c").bitcast(I32))
+        w2_w = held([P, 2, H // 2], I32, "w2_w")
+        nc.sync.dma_start(out=w2_w[:], in_=w2_words.rearrange("a p c -> p a c").bitcast(I32))
+        tab_w.append(load_table(1))
+
+        w1_raw = {}
+        w1_raw[0, 0] = load_rows(w1, 0, 0, 0)
+        w1_raw[1, 0] = load_rows(w1, 1, 0, 1, 2)
         wgt_t = held([P, M], F32, "wgt_t")
         nc.sync.dma_start(out=wgt_t[:], in_=wgt)
         sv_t = load_vec(sv, "sv_t")
         gu_t = load_vec(gu, "gu_t")
-        w1_raw[0, 1] = load_rows(w1, 0, 1)
-        w1_raw[1, 1] = load_rows(w1, 1, 1)
-        w3_raw = [load_rows(w3, a, 0) for a in range(2)]
+        w1_raw[0, 1] = load_rows(w1, 0, 1, 2)
+        w1_raw[1, 1] = load_rows(w1, 1, 1, 3)
+        w3_raw = [load_rows(w3, a, 0, 1 + 3 * a) for a in range(2)]
         w4_w = held([P, 2, N], I32, "w4_w")
         nc.sync.dma_start(out=w4_w[:], in_=w4_words.rearrange("a p c i -> p a (c i)").bitcast(I32))
+        for q in range(4):
+            nc.sync.dma_start(out=w4_sc[:].bitcast(I32)[32 * q:32 * q + 8, :],
+                              in_=w4_scales[:, 4 * q:4 * q + 4, :].bitcast(I32))
         list3 = keep.tile([P, M // PER_COL], U16, name="list3")
         nc.sync.dma_start(list3[:], offs3)
         wgo_t = held([P, M], F32, "wgo_t")
         nc.sync.dma_start(out=wgo_t[:], in_=wgo)
 
-        def place_rows(queue, plane, rows, first, count):
-            for q in range(4):
-                queue.dma_start(out=plane[:].bitcast(I32)[32 * q:32 * q + 4],
-                                in_=rows[:].bitcast(I32)[first + count * q:first + count * (q + 1), :])
-
-        dealt_sc = held([P, KP], U8, "dealt_sc")
-        nc.vector.tensor_copy(out=dealt_sc[:].rearrange("p (t m) -> p t m", t=PACK),
-                              in_=w_sc[:].rearrange("p (m t) -> p t m", t=PACK))
-        place_rows(nc.gpsimd, w2p_sc, dealt_sc, 0, 16)
-        picked_sc = held([P, S], U8, "picked_sc")
-        nc.vector.tensor_copy(out=picked_sc[:], in_=tab_sc[:].indirect(list1[:]))
-        place_rows(nc.gpsimd, v_sc, picked_sc, 0, 8)
+        v_sc0 = held([P, S], U8, "v_sc0")
+        nc.vector.tensor_copy(out=v_sc0[:], in_=tab_sc[:].indirect(list1[:]))
+        nc.scalar.dma_start(out=v_sc1[:].bitcast(I32)[0:112, :], in_=v_sc0[:].bitcast(I32)[16:128, :])
+        v_sc = [v_sc0, v_sc1]
         v_w = {}
 
         def gather_words(a, c):
@@ -122,32 +127,41 @@ def tile_list_stigma_purity_scores_kernel(
 
         gather_words(0, 0)
         gather_words(0, 1)
-        gather_words(1, 0)
-        gather_words(1, 1)
+        w2p = {}
+        w2p_sc = {}
 
-        w2p = []
-        for b in range(2):
+        def deal_w2(b):
+            sp = held([P, 2, KP], U8, "w2p_sc%d" % b)
+            nc.vector.tensor_copy(out=sp[:].rearrange("p a (t m) -> p a t m", t=PACK),
+                                  in_=w2_sc[:, :, b * KP:(b + 1) * KP].rearrange("p a (m t) -> p a t m", t=PACK))
             wp = held([P, 2, 2 * KP], U8, "w2p%d" % b)
             src = w2_w[:].bitcast(U16)[:, :, b * KP:(b + 1) * KP]
             nc.vector.tensor_copy(out=wp[:].bitcast(U16).rearrange("p a (t m) -> p a t m", t=PACK),
                                   in_=src.rearrange("p a (m t) -> p a t m", t=PACK))
-            w2p.append(wp)
+            w2p[b] = wp
+            w2p_sc[b] = sp
+
+        deal_w2(0)
+        gather_words(1, 0)
+        gather_words(1, 1)
 
         nga = held([P, 2, PACK], F32, "nga")
         nc.vector.tensor_scalar(out=nga[:], in0=ga_t[:], scalar1=-1.0, scalar2=None, op0=ALU.mult)
 
-        def cast(raw, vector_cols):
-            grouped = ring.tile([P, KP * PACK], BF16, name="grouped", align_bytes=64, bufs=3)
+        def grouped_tile():
+            return ring.tile([P, KP * PACK], BF16, name="grouped", align_bytes=64, bufs=3)
+
+        def cast(copy, grouped, raw, half):
+            cols = slice(half * P // 2, (half + 1) * P // 2)
             dst = grouped[:].rearrange("p (t m j) -> p m j t", t=PACK, j=PACK)
             src = raw[:].rearrange("p j (m t) -> p m j t", t=PACK)
-            if vector_cols > 0:
-                nc.vector.tensor_copy(out=dst[:, :vector_cols], in_=src[:, :vector_cols])
-            if vector_cols < P:
-                nc.scalar.copy(out=dst[:, vector_cols:], in_=src[:, vector_cols:])
-            return grouped
+            copy(out=dst[:, cols], in_=src[:, cols])
 
-        def quantize(grouped, width, name):
-            codes = held([P, width], U32, name + "_w")
+        def quantize(grouped, width, name, place=None):
+            if place is None:
+                codes = held([P, width], U32, name + "_w")
+            else:
+                codes = arena.tile([P, width], U32, name=name + "_w", align_bytes=64, offset=place)
             scales = held([P, width], U8, name + "_s")
             nc.vector.quantize_mx(out=codes[:].bitcast(FP8X4), scales=scales[:], in_=grouped[:])
             return codes, scales
@@ -155,16 +169,19 @@ def tile_list_stigma_purity_scores_kernel(
         h = {}
 
         def foreign(b, i):
-            ht = held([P, S], F32, "h%d%d" % (b, i))
+            if b == 0 and i < 2:
+                ht = arena.tile([P, S], F32, name="h%d%d" % (b, i), align_bytes=64, offset=4096 * i)
+            else:
+                ht = held([P, S], F32, "h%d%d" % (b, i))
             for c in range(2):
                 cols = slice(c * BANK, (c + 1) * BANK)
-                acc = psum.tile([P, BANK], F32, name="acc_s")
+                acc = psum.tile([P, BANK], F32, name="acc_s", bufs=3)
                 for a in range(2):
                     nc.tensor.matmul_mx(
                         out=acc[:],
                         lhsT=w2p[b][:, a, 2 * P * i:2 * P * (i + 1)].bitcast(FP4X4),
-                        lhsT_scale=w2p_sc[:, 2 * b + a, P * i:P * (i + 1)],
-                        rhs=v_w[a, c][:].bitcast(FP8X4), rhs_scale=v_sc[:, a, cols],
+                        lhsT_scale=w2p_sc[b][:, a, P * i:P * (i + 1)],
+                        rhs=v_w[a, c][:].bitcast(FP8X4), rhs_scale=v_sc[a][:, cols],
                         start=(a == 0), stop=(a == 1))
                 nc.scalar.activation(out=ht[:, cols], in_=acc[:], func=ACT.Abs)
             h[b, i] = ht
@@ -175,28 +192,37 @@ def tile_list_stigma_purity_scores_kernel(
             ht = h[b, i]
             for c in range(2):
                 cols = slice(c * BANK, (c + 1) * BANK)
-                acc = psum.tile([P, BANK], F32, name="acc_v")
+                acc = psum.tile([P, BANK], F32, name="acc_v", bufs=5)
                 for a in range(2):
                     codes, scales = w1q[a, b]
                     nc.tensor.matmul_mx(
                         out=acc[:],
                         lhsT=codes[:, P * i:P * (i + 1)].bitcast(FP8X4),
                         lhsT_scale=scales[:, P * i:P * (i + 1)],
-                        rhs=v_w[a, c][:].bitcast(FP8X4), rhs_scale=v_sc[:, a, cols],
+                        rhs=v_w[a, c][:].bitcast(FP8X4), rhs_scale=v_sc[a][:, cols],
                         start=(a == 0), stop=(a == 1))
                 nc.vector.scalar_tensor_tensor(out=ht[:, cols], in0=ht[:, cols], scalar=nga[:, b, i:i + 1],
                                                in1=acc[:], op0=ALU.mult, op1=ALU.add)
 
         planes = {}
 
+        zs = {}
+
         def pick(b, i, u):
-            if i == 0:
-                planes[b, u] = ring.tile([P, PACK, HALF], BF16, name="xs", align_bytes=64)
             cols = HALF // PER_COL
-            z = ring.tile([P, HALF], F32, name="z", align_bytes=64, bufs=8)
+            if b == 1 and u == 1:
+                z = arena.tile([P, HALF], F32, name="z%d" % i, align_bytes=64, offset=5 * 8192 + 1024 * i)
+            else:
+                z = ring.tile([P, HALF], F32, name="z", align_bytes=64, bufs=12)
             nc.vector.tensor_tensor(out=z[:], in0=h[b, i][:].indirect(list2[:, u * cols:(u + 1) * cols]),
                                     in1=wgt_t[:, u * HALF:(u + 1) * HALF], op=ALU.mult)
-            th = ring.tile([P, HALF], F32, name="th", align_bytes=64)
+            zs[b, i, u] = z
+
+        def squash(b, i, u):
+            if i == 0:
+                planes[b, u] = ring.tile([P, PACK, HALF], BF16, name="xs", align_bytes=64)
+            z = zs[b, i, u]
+            th = ring.tile([P, HALF], F32, name="th", align_bytes=64, bufs=2)
             nc.scalar.activation(out=th[:], in_=z[:], func=ACT.Tanh, scale=sv_t[:, b, i:i + 1])
             nc.scalar.activation(out=planes[b, u][:, i, :], in_=th[:], func=ACT.Copy, scale=gu_t[:, b, i:i + 1])
 
@@ -204,61 +230,74 @@ def tile_list_stigma_purity_scores_kernel(
 
         def features(b, u):
             xi = ring.tile([P, HALF * PACK], BF16, name="xi", align_bytes=64, bufs=2)
-            nc.vector.tensor_copy(out=xi[:].rearrange("p (c e t) -> p c t e", e=4, t=PACK),
+            weave = nc.vector.tensor_copy if u == 0 else nc.scalar.copy
+            weave(out=xi[:].rearrange("p (c e t) -> p c t e", e=4, t=PACK),
                                   in_=planes[b, u][:].rearrange("p t (c e) -> p c t e", e=4))
             xq[b, u] = quantize(xi, HALF, "x%d%d" % (b, u))
 
-        g00 = cast(w1_raw[0, 0], 0)
-        g10 = cast(w1_raw[1, 0], P // 2)
-        for i in range(PACK):
-            foreign(0, i)
+        g00 = grouped_tile()
+        cast(nc.scalar.copy, g00, w1_raw[0, 0], 0)
+        cast(nc.scalar.copy, g00, w1_raw[0, 0], 1)
+        g10 = grouped_tile()
+        cast(nc.vector.tensor_copy, g10, w1_raw[1, 0], 0)
         w1q[0, 0] = quantize(g00, KP, "w1q00")
+        cast(nc.vector.tensor_copy, g10, w1_raw[1, 0], 1)
+        foreign(0, 0)
         w1q[1, 0] = quantize(g10, KP, "w1q10")
+        deal_w2(1)
 
-        g01 = cast(w1_raw[0, 1], 0)
         stigma(0, 0)
+        foreign(0, 1)
         pick(0, 0, 0)
-        g11 = cast(w1_raw[1, 1], 0)
+        g01 = grouped_tile()
+        cast(nc.scalar.copy, g01, w1_raw[0, 1], 0)
         stigma(0, 1)
-        w1q[0, 1] = quantize(g01, KP, "w1q01")
+        foreign(0, 2)
         pick(0, 1, 0)
-        foreign(1, 0)
+        cast(nc.scalar.copy, g01, w1_raw[0, 1], 1)
+        g11 = grouped_tile()
+        cast(nc.scalar.copy, g11, w1_raw[1, 1], 0)
         stigma(0, 2)
+        foreign(0, 3)
+        w1q[0, 1] = quantize(g01, KP, "w1q01", 5 * 8192)
         pick(0, 2, 0)
-        foreign(1, 1)
+        cast(nc.scalar.copy, g11, w1_raw[1, 1], 1)
         stigma(0, 3)
-        w1q[1, 1] = quantize(g11, KP, "w1q11")
+        foreign(1, 0)
+        w1q[1, 1] = quantize(g11, KP, "w1q11", 5 * 8192 + 2048)
         pick(0, 3, 0)
-        foreign(1, 2)
-        stigma(1, 0)
-        features(0, 0)
-        pick(1, 0, 0)
-        foreign(1, 3)
-        g3 = [cast(w3_raw[0], 0)]
-        stigma(1, 1)
-        pick(1, 1, 0)
-        g3.append(cast(w3_raw[1], 0))
-        stigma(1, 2)
-        pick(1, 2, 0)
-        stigma(1, 3)
-        pick(1, 3, 0)
+        g3 = []
+        for i in range(PACK):
+            stigma(1, i)
+            if i + 1 < PACK:
+                foreign(1, i + 1)
+            pick(1, i, 0)
+            if i % 2 == 0:
+                g3.append(grouped_tile())
+            cast(nc.scalar.copy, g3[i // 2], w3_raw[i // 2], i % 2)
+            squash(0, i, 0)
         w3q = [quantize(g3[a], N, "w3q%d" % a) for a in range(2)]
+        features(0, 0)
+        for i in range(PACK):
+            squash(1, i, 0)
 
-        place_rows(nc.sync, w4p_sc, dealt_sc, 64, 8)
         w4p = held([P, 2, N], I32, "w4p")
         nc.vector.tensor_copy(out=w4p[:].rearrange("p a (t m) -> p a m t", t=PACK),
                               in_=w4_w[:].rearrange("p a (m t) -> p a m t", t=PACK))
+        w4p_sc = held([P, N], U8, "w4p_sc")
+        nc.vector.tensor_copy(out=w4p_sc[:].rearrange("p (t m) -> p t m", t=PACK),
+                              in_=w4_sc[:].rearrange("p (m t) -> p t m", t=PACK))
 
         pages = [keep.tile([P, SLOTS], F32, name="page%d" % i, tag=tag, align_bytes=64)
-                 for i, tag in enumerate(("page0", "tab_w0", "tab_w1", "w2_w"))]
+                 for i, tag in enumerate(("page0", "page1", "page2", "page3"))]
         for page in pages:
             nc.vector.memset(page[:], 0.0)
 
         ys = {}
 
         def scores(u, pair):
-            acc3 = psum.tile([P, BANK], F32, name="acc_s")
-            acc4 = psum.tile([P, BANK], F32, name="acc_v")
+            acc3 = psum.tile([P, BANK], F32, name="acc_s", bufs=3)
+            acc4 = psum.tile([P, BANK], F32, name="acc_v", bufs=5)
             for e in range(2):
                 i = 2 * pair + e
                 cols = slice(e * HALF, (e + 1) * HALF)
@@ -276,7 +315,7 @@ def tile_list_stigma_purity_scores_kernel(
                     nc.tensor.matmul_mx(
                         out=acc4[:, cols],
                         lhsT=w4p[:, a, P * i:P * (i + 1)].bitcast(FP8X4),
-                        lhsT_scale=w4p_sc[:, a, P * i:P * (i + 1)],
+                        lhsT_scale=w4p_sc[4 * a:P, P * i:P * (i + 1)],
                         rhs=xq[a, u][0][:].bitcast(FP8X4), rhs_scale=xq[a, u][1][:],
                         start=(a == 0), stop=(a == 1))
             y3 = ring.tile([P, BANK], F32, name="y3", align_bytes=64, bufs=2)
@@ -300,10 +339,13 @@ def tile_list_stigma_purity_scores_kernel(
         features(1, 0)
         for i in range(PACK):
             pick(1, i, 1)
-        features(0, 1)
         scores(0, 0)
         scores(0, 1)
+        for b in range(2):
+            for i in range(PACK):
+                squash(b, i, 1)
         file_scores(0, 0)
+        features(0, 1)
         features(1, 1)
         file_scores(0, 1)
         file_scores(0, 2)

@@ -81,9 +81,10 @@ def tile_list_stigma_purity_scores_kernel(
 
         list1 = keep.tile([P, S // PER_COL], U16, name="list1")
         nc.sync.dma_start(list1[:], offs)
-        ga_t = load_vec(ga, "ga_t")
         list2 = keep.tile([P, M // PER_COL], U16, name="list2")
         nc.sync.dma_start(list2[:], offs2)
+        list3 = keep.tile([P, M // PER_COL], U16, name="list3")
+        nc.sync.dma_start(list3[:], offs3)
         load_scale_rows(nc.sync, tab_sc, tab_scales)
         tab_w = [load_table(0)]
         for q in range(4):
@@ -91,10 +92,10 @@ def tile_list_stigma_purity_scores_kernel(
                               in_=w2_scales[:, 4 * q:4 * q + 4, :].rearrange("a r c -> r a c").bitcast(I32))
         w2_w = held([P, 2, H // 2], I32, "w2_w")
         nc.sync.dma_start(out=w2_w[:], in_=w2_words.rearrange("a p c -> p a c").bitcast(I32))
-        tab_w.append(load_table(1))
-
         w1_raw = {}
         w1_raw[0, 0] = load_rows(w1, 0, 0, 0)
+        tab_w.append(load_table(1))
+        ga_t = load_vec(ga, "ga_t")
         w1_raw[1, 0] = load_rows(w1, 1, 0, 1, 2)
         wgt_t = held([P, M], F32, "wgt_t")
         nc.sync.dma_start(out=wgt_t[:], in_=wgt)
@@ -102,14 +103,12 @@ def tile_list_stigma_purity_scores_kernel(
         gu_t = load_vec(gu, "gu_t")
         w1_raw[0, 1] = load_rows(w1, 0, 1, 2)
         w1_raw[1, 1] = load_rows(w1, 1, 1, 3)
-        w3_raw = [load_rows(w3, a, 0, 1 + 3 * a) for a in range(2)]
+        w3_raw = [load_rows(w3, a, 0, 4 * a) for a in range(2)]
         w4_w = held([P, 2, N], I32, "w4_w")
         nc.sync.dma_start(out=w4_w[:], in_=w4_words.rearrange("a p c i -> p a (c i)").bitcast(I32))
         for q in range(4):
             nc.sync.dma_start(out=w4_sc[:].bitcast(I32)[32 * q:32 * q + 8, :],
                               in_=w4_scales[:, 4 * q:4 * q + 4, :].bitcast(I32))
-        list3 = keep.tile([P, M // PER_COL], U16, name="list3")
-        nc.sync.dma_start(list3[:], offs3)
         wgo_t = held([P, M], F32, "wgo_t")
         nc.sync.dma_start(out=wgo_t[:], in_=wgo)
 
@@ -131,10 +130,14 @@ def tile_list_stigma_purity_scores_kernel(
         w2p_sc = {}
 
         def deal_w2(b):
-            sp = held([P, 2, KP], U8, "w2p_sc%d" % b)
+            if b == 0:
+                sp = held([P, 2, KP], U8, "w2p_sc0")
+                wp = held([P, 2, 2 * KP], U8, "w2p0")
+            else:
+                sp = arena.tile([P, 2, KP], U8, name="w2p_sc1", align_bytes=64, offset=6 * 8192)
+                wp = arena.tile([P, 2, 2 * KP], U8, name="w2p1", align_bytes=64, offset=6 * 8192 + 2048)
             nc.vector.tensor_copy(out=sp[:].rearrange("p a (t m) -> p a t m", t=PACK),
                                   in_=w2_sc[:, :, b * KP:(b + 1) * KP].rearrange("p a (m t) -> p a t m", t=PACK))
-            wp = held([P, 2, 2 * KP], U8, "w2p%d" % b)
             src = w2_w[:].bitcast(U16)[:, :, b * KP:(b + 1) * KP]
             nc.vector.tensor_copy(out=wp[:].bitcast(U16).rearrange("p a (t m) -> p a t m", t=PACK),
                                   in_=src.rearrange("p a (m t) -> p a t m", t=PACK))
@@ -146,7 +149,7 @@ def tile_list_stigma_purity_scores_kernel(
         gather_words(1, 1)
 
         nga = held([P, 2, PACK], F32, "nga")
-        nc.vector.tensor_scalar(out=nga[:], in0=ga_t[:], scalar1=-1.0, scalar2=None, op0=ALU.mult)
+        nc.gpsimd.tensor_scalar(out=nga[:], in0=ga_t[:], scalar1=-1.0, scalar2=None, op0=ALU.mult)
 
         def grouped_tile():
             return ring.tile([P, KP * PACK], BF16, name="grouped", align_bytes=64, bufs=3)
@@ -170,7 +173,7 @@ def tile_list_stigma_purity_scores_kernel(
 
         def foreign(b, i):
             if b == 0 and i < 2:
-                ht = arena.tile([P, S], F32, name="h%d%d" % (b, i), align_bytes=64, offset=4096 * i)
+                ht = arena.tile([P, S], F32, name="h%d%d" % (b, i), align_bytes=64, offset=8192 + 4096 * i)
             else:
                 ht = held([P, S], F32, "h%d%d" % (b, i))
             for c in range(2):
@@ -204,82 +207,89 @@ def tile_list_stigma_purity_scores_kernel(
                 nc.vector.scalar_tensor_tensor(out=ht[:, cols], in0=ht[:, cols], scalar=nga[:, b, i:i + 1],
                                                in1=acc[:], op0=ALU.mult, op1=ALU.add)
 
-        planes = {}
-
         zs = {}
 
-        def pick(b, i, u):
-            cols = HALF // PER_COL
-            if b == 1 and u == 1:
-                z = arena.tile([P, HALF], F32, name="z%d" % i, align_bytes=64, offset=5 * 8192 + 1024 * i)
+        def pick(b, i, first, width, place=None):
+            if place is None:
+                z = ring.tile([P, width], F32, name="z%d" % width, align_bytes=64)
             else:
-                z = ring.tile([P, HALF], F32, name="z", align_bytes=64, bufs=12)
-            nc.vector.tensor_tensor(out=z[:], in0=h[b, i][:].indirect(list2[:, u * cols:(u + 1) * cols]),
-                                    in1=wgt_t[:, u * HALF:(u + 1) * HALF], op=ALU.mult)
-            zs[b, i, u] = z
+                z = arena.tile([P, width], F32, name="late_z%d" % i, align_bytes=64, offset=place)
+            entries = list2[:, first // PER_COL:(first + width) // PER_COL]
+            nc.vector.tensor_tensor(out=z[:], in0=h[b, i][:].indirect(entries),
+                                    in1=wgt_t[:, first:first + width], op=ALU.mult)
+            zs[b, i, first] = z
 
-        def squash(b, i, u):
-            if i == 0:
-                planes[b, u] = ring.tile([P, PACK, HALF], BF16, name="xs", align_bytes=64)
-            z = zs[b, i, u]
-            th = ring.tile([P, HALF], F32, name="th", align_bytes=64, bufs=2)
-            nc.scalar.activation(out=th[:], in_=z[:], func=ACT.Tanh, scale=sv_t[:, b, i:i + 1])
-            nc.scalar.activation(out=planes[b, u][:, i, :], in_=th[:], func=ACT.Copy, scale=gu_t[:, b, i:i + 1])
+        planes = [held([P, PACK, M], BF16, "x_rows%d" % b) for b in range(2)]
 
+        def squash(b, i, first, width):
+            th = ring.tile([P, width], F32, name="th", align_bytes=64, bufs=2)
+            nc.scalar.activation(out=th[:], in_=zs[b, i, first][:], func=ACT.Tanh, scale=sv_t[:, b, i:i + 1])
+            nc.scalar.activation(out=planes[b][:, i, first:first + width], in_=th[:], func=ACT.Copy,
+                                 scale=gu_t[:, b, i:i + 1])
+
+        woven = {}
         xq = {}
 
-        def features(b, u):
-            xi = ring.tile([P, HALF * PACK], BF16, name="xi", align_bytes=64, bufs=2)
-            weave = nc.vector.tensor_copy if u == 0 else nc.scalar.copy
-            weave(out=xi[:].rearrange("p (c e t) -> p c t e", e=4, t=PACK),
-                                  in_=planes[b, u][:].rearrange("p t (c e) -> p c t e", e=4))
-            xq[b, u] = quantize(xi, HALF, "x%d%d" % (b, u))
+        def weave(copy, b, u):
+            xi = ring.tile([P, HALF * PACK], BF16, name="xi", align_bytes=64)
+            copy(out=xi[:].rearrange("p (c e t) -> p c t e", e=4, t=PACK),
+                 in_=planes[b][:, :, u * HALF:(u + 1) * HALF].rearrange("p t (c e) -> p c t e", e=4))
+            woven[b, u] = xi
 
-        g00 = grouped_tile()
-        cast(nc.scalar.copy, g00, w1_raw[0, 0], 0)
-        cast(nc.scalar.copy, g00, w1_raw[0, 0], 1)
-        g10 = grouped_tile()
-        cast(nc.vector.tensor_copy, g10, w1_raw[1, 0], 0)
-        w1q[0, 0] = quantize(g00, KP, "w1q00")
-        cast(nc.vector.tensor_copy, g10, w1_raw[1, 0], 1)
+        def features(b, u):
+            xq[b, u] = quantize(woven[b, u], HALF, "x%d%d" % (b, u))
+
+        def cast_whole(raw, grouped):
+            for half in range(2):
+                cast(nc.scalar.copy, grouped, raw, half)
+            return grouped
+
+        g00 = cast_whole(w1_raw[0, 0], grouped_tile())
+        g10 = cast_whole(w1_raw[1, 0], arena.tile([P, KP * PACK], BF16, name="g10", align_bytes=64, offset=6 * 8192))
         foreign(0, 0)
+        w1q[0, 0] = quantize(g00, KP, "w1q00")
         w1q[1, 0] = quantize(g10, KP, "w1q10")
         deal_w2(1)
 
+        late = 5 * 8192
+        g1 = [grouped_tile(), grouped_tile()]
         stigma(0, 0)
         foreign(0, 1)
-        pick(0, 0, 0)
-        g01 = grouped_tile()
-        cast(nc.scalar.copy, g01, w1_raw[0, 1], 0)
+        cast(nc.scalar.copy, g1[0], w1_raw[0, 1], 0)
         stigma(0, 1)
         foreign(0, 2)
-        pick(0, 1, 0)
-        cast(nc.scalar.copy, g01, w1_raw[0, 1], 1)
-        g11 = grouped_tile()
-        cast(nc.scalar.copy, g11, w1_raw[1, 1], 0)
+        pick(0, 0, 0, M)
+        cast(nc.scalar.copy, g1[0], w1_raw[0, 1], 1)
+        cast(nc.scalar.copy, g1[1], w1_raw[1, 1], 0)
         stigma(0, 2)
         foreign(0, 3)
-        w1q[0, 1] = quantize(g01, KP, "w1q01", 5 * 8192)
-        pick(0, 2, 0)
-        cast(nc.scalar.copy, g11, w1_raw[1, 1], 1)
+        w1q[0, 1] = quantize(g1[0], KP, "w1q01", late)
+        pick(0, 1, 0, M)
+        cast(nc.scalar.copy, g1[1], w1_raw[1, 1], 1)
         stigma(0, 3)
         foreign(1, 0)
-        w1q[1, 1] = quantize(g11, KP, "w1q11", 5 * 8192 + 2048)
-        pick(0, 3, 0)
+        w1q[1, 1] = quantize(g1[1], KP, "w1q11", late + 2048)
+        pick(0, 2, 0, M)
         g3 = []
         for i in range(PACK):
             stigma(1, i)
             if i + 1 < PACK:
                 foreign(1, i + 1)
-            pick(1, i, 0)
+            if i == 0:
+                pick(0, 3, 0, M)
+            else:
+                pick(1, i - 1, 0, HALF)
             if i % 2 == 0:
                 g3.append(grouped_tile())
             cast(nc.scalar.copy, g3[i // 2], w3_raw[i // 2], i % 2)
-            squash(0, i, 0)
-        w3q = [quantize(g3[a], N, "w3q%d" % a) for a in range(2)]
+            squash(0, i, 0, M)
+        w3q = [quantize(g3[0], N, "w3q0")]
+        pick(1, PACK - 1, 0, HALF)
+        weave(nc.vector.tensor_copy, 0, 0)
+        w3q.append(quantize(g3[1], N, "w3q1"))
         features(0, 0)
         for i in range(PACK):
-            squash(1, i, 0)
+            squash(1, i, 0, HALF)
 
         w4p = held([P, 2, N], I32, "w4p")
         nc.vector.tensor_copy(out=w4p[:].rearrange("p a (t m) -> p a m t", t=PACK),
@@ -334,16 +344,17 @@ def tile_list_stigma_purity_scores_kernel(
             if u == 1:
                 nc.sync.dma_start(out=rows_out[:, i, :], in_=pages[i][:])
 
-        for i in range(PACK):
-            pick(0, i, 1)
+        weave(nc.vector.tensor_copy, 1, 0)
+        pick(1, 0, HALF, HALF, late)
         features(1, 0)
-        for i in range(PACK):
-            pick(1, i, 1)
+        for i in range(1, PACK):
+            pick(1, i, HALF, HALF, late + 1024 * i)
         scores(0, 0)
         scores(0, 1)
-        for b in range(2):
-            for i in range(PACK):
-                squash(b, i, 1)
+        weave(nc.scalar.copy, 0, 1)
+        for i in range(PACK):
+            squash(1, i, HALF, HALF)
+        weave(nc.scalar.copy, 1, 1)
         file_scores(0, 0)
         features(0, 1)
         features(1, 1)

@@ -81,10 +81,9 @@ def tile_list_stigma_purity_scores_kernel(
 
         list1 = keep.tile([P, S // PER_COL], U16, name="list1")
         nc.sync.dma_start(list1[:], offs)
-        list2 = keep.tile([P, M // PER_COL], U16, name="list2")
-        nc.sync.dma_start(list2[:], offs2)
-        list3 = keep.tile([P, M // PER_COL], U16, name="list3")
-        nc.sync.dma_start(list3[:], offs3)
+        wgt_t = held([P, M], F32, "wgt_t")
+        nc.sync.dma_start(out=wgt_t[:], in_=wgt)
+        sv_t = load_vec(sv, "sv_t")
         load_scale_rows(nc.sync, tab_sc, tab_scales)
         tab_w = [load_table(0)]
         for q in range(4):
@@ -97,20 +96,27 @@ def tile_list_stigma_purity_scores_kernel(
         tab_w.append(load_table(1))
         ga_t = load_vec(ga, "ga_t")
         w1_raw[1, 0] = load_rows(w1, 1, 0, 1, 2)
-        wgt_t = held([P, M], F32, "wgt_t")
-        nc.sync.dma_start(out=wgt_t[:], in_=wgt)
-        sv_t = load_vec(sv, "sv_t")
+        list2 = keep.tile([P, M // PER_COL], U16, name="list2")
+        nc.sync.dma_start(list2[:], offs2)
         gu_t = load_vec(gu, "gu_t")
         w1_raw[0, 1] = load_rows(w1, 0, 1, 2)
         w1_raw[1, 1] = load_rows(w1, 1, 1, 3)
-        w3_raw = [load_rows(w3, a, 0, 4 * a) for a in range(2)]
+        w3_raw = [load_rows(w3, a, 0, 1 + 3 * a) for a in range(2)]
         w4_w = held([P, 2, N], I32, "w4_w")
         nc.sync.dma_start(out=w4_w[:], in_=w4_words.rearrange("a p c i -> p a (c i)").bitcast(I32))
         for q in range(4):
             nc.sync.dma_start(out=w4_sc[:].bitcast(I32)[32 * q:32 * q + 8, :],
                               in_=w4_scales[:, 4 * q:4 * q + 4, :].bitcast(I32))
+        list3 = keep.tile([P, M // PER_COL], U16, name="list3")
+        nc.sync.dma_start(list3[:], offs3)
         wgo_t = held([P, M], F32, "wgo_t")
         nc.sync.dma_start(out=wgo_t[:], in_=wgo)
+
+        gains = {}
+        for b in range(2):
+            for i in range(PACK):
+                gains[b, i] = held([P, M], F32, "gain%d%d" % (b, i))
+                nc.scalar.activation(out=gains[b, i][:], in_=wgt_t[:], func=ACT.Copy, scale=sv_t[:, b, i:i + 1])
 
         v_sc0 = held([P, S], U8, "v_sc0")
         nc.vector.tensor_copy(out=v_sc0[:], in_=tab_sc[:].indirect(list1[:]))
@@ -173,7 +179,7 @@ def tile_list_stigma_purity_scores_kernel(
 
         def foreign(b, i):
             if b == 0 and i < 2:
-                ht = arena.tile([P, S], F32, name="h%d%d" % (b, i), align_bytes=64, offset=8192 + 4096 * i)
+                ht = arena.tile([P, S], F32, name="h%d%d" % (b, i), align_bytes=64, offset=4096 * i)
             else:
                 ht = held([P, S], F32, "h%d%d" % (b, i))
             for c in range(2):
@@ -207,37 +213,37 @@ def tile_list_stigma_purity_scores_kernel(
                 nc.vector.scalar_tensor_tensor(out=ht[:, cols], in0=ht[:, cols], scalar=nga[:, b, i:i + 1],
                                                in1=acc[:], op0=ALU.mult, op1=ALU.add)
 
+        late = 5 * 8192
         zs = {}
+        for b in range(2):
+            for u in range(2):
+                if b == 1 and u == 1:
+                    zs[b, u] = arena.tile([P, PACK, HALF], F32, name="late_z", align_bytes=64, offset=late)
+                else:
+                    zs[b, u] = held([P, PACK, HALF], F32, "z%d%d" % (b, u))
 
-        def pick(b, i, first, width, place=None):
-            if place is None:
-                z = ring.tile([P, width], F32, name="z%d" % width, align_bytes=64)
-            else:
-                z = arena.tile([P, width], F32, name="late_z%d" % i, align_bytes=64, offset=place)
-            entries = list2[:, first // PER_COL:(first + width) // PER_COL]
-            nc.vector.tensor_tensor(out=z[:], in0=h[b, i][:].indirect(entries),
-                                    in1=wgt_t[:, first:first + width], op=ALU.mult)
-            zs[b, i, first] = z
+        def pick(b, i, u):
+            entries = list2[:, u * HALF // PER_COL:(u + 1) * HALF // PER_COL]
+            nc.vector.tensor_tensor(out=zs[b, u][:, i, :], in0=h[b, i][:].indirect(entries),
+                                    in1=gains[b, i][:, u * HALF:(u + 1) * HALF], op=ALU.mult)
 
-        planes = [held([P, PACK, M], BF16, "x_rows%d" % b) for b in range(2)]
-
-        def squash(b, i, first, width):
-            th = ring.tile([P, width], F32, name="th", align_bytes=64, bufs=2)
-            nc.scalar.activation(out=th[:], in_=zs[b, i, first][:], func=ACT.Tanh, scale=sv_t[:, b, i:i + 1])
-            nc.scalar.activation(out=planes[b][:, i, first:first + width], in_=th[:], func=ACT.Copy,
-                                 scale=gu_t[:, b, i:i + 1])
-
-        woven = {}
+        squashed = {}
+        rounded = {}
         xq = {}
 
-        def weave(copy, b, u):
-            xi = ring.tile([P, HALF * PACK], BF16, name="xi", align_bytes=64)
-            copy(out=xi[:].rearrange("p (c e t) -> p c t e", e=4, t=PACK),
-                 in_=planes[b][:, :, u * HALF:(u + 1) * HALF].rearrange("p t (c e) -> p c t e", e=4))
-            woven[b, u] = xi
+        def squash(b, u):
+            th = ring.tile([P, HALF, PACK], F32, name="th", align_bytes=64, bufs=2)
+            nc.scalar.activation(out=th[:], in_=zs[b, u][:].rearrange("p t m -> p m t"), func=ACT.Tanh)
+            squashed[b, u] = th
+
+        def scale_round(b, u):
+            xi = ring.tile([P, HALF * PACK], BF16, name="xi", align_bytes=64, bufs=2)
+            nc.vector.tensor_tensor(out=xi[:].rearrange("p (m t) -> p m t", t=PACK), in0=squashed[b, u][:],
+                                    in1=gu_t[:, b, :].unsqueeze(1).to_broadcast([P, HALF, PACK]), op=ALU.mult)
+            rounded[b, u] = xi
 
         def features(b, u):
-            xq[b, u] = quantize(woven[b, u], HALF, "x%d%d" % (b, u))
+            xq[b, u] = quantize(rounded[b, u], HALF, "x%d%d" % (b, u))
 
         def cast_whole(raw, grouped):
             for half in range(2):
@@ -245,51 +251,53 @@ def tile_list_stigma_purity_scores_kernel(
             return grouped
 
         g00 = cast_whole(w1_raw[0, 0], grouped_tile())
-        g10 = cast_whole(w1_raw[1, 0], arena.tile([P, KP * PACK], BF16, name="g10", align_bytes=64, offset=6 * 8192))
-        foreign(0, 0)
+        g10 = arena.tile([P, KP * PACK], BF16, name="g10", align_bytes=64, offset=6 * 8192)
+        cast(nc.vector.tensor_copy, g10, w1_raw[1, 0], 0)
         w1q[0, 0] = quantize(g00, KP, "w1q00")
+        cast(nc.vector.tensor_copy, g10, w1_raw[1, 0], 1)
+        foreign(0, 0)
         w1q[1, 0] = quantize(g10, KP, "w1q10")
         deal_w2(1)
 
-        late = 5 * 8192
         g1 = [grouped_tile(), grouped_tile()]
         stigma(0, 0)
         foreign(0, 1)
         cast(nc.scalar.copy, g1[0], w1_raw[0, 1], 0)
         stigma(0, 1)
         foreign(0, 2)
-        pick(0, 0, 0, M)
+        pick(0, 0, 0)
         cast(nc.scalar.copy, g1[0], w1_raw[0, 1], 1)
         cast(nc.scalar.copy, g1[1], w1_raw[1, 1], 0)
         stigma(0, 2)
         foreign(0, 3)
         w1q[0, 1] = quantize(g1[0], KP, "w1q01", late)
-        pick(0, 1, 0, M)
+        pick(0, 1, 0)
         cast(nc.scalar.copy, g1[1], w1_raw[1, 1], 1)
         stigma(0, 3)
         foreign(1, 0)
         w1q[1, 1] = quantize(g1[1], KP, "w1q11", late + 2048)
-        pick(0, 2, 0, M)
+        pick(0, 2, 0)
         g3 = []
         for i in range(PACK):
             stigma(1, i)
             if i + 1 < PACK:
                 foreign(1, i + 1)
             if i == 0:
-                pick(0, 3, 0, M)
+                pick(0, 3, 0)
             else:
-                pick(1, i - 1, 0, HALF)
+                pick(1, i - 1, 0)
             if i % 2 == 0:
                 g3.append(grouped_tile())
             cast(nc.scalar.copy, g3[i // 2], w3_raw[i // 2], i % 2)
-            squash(0, i, 0, M)
+        squash(0, 0)
         w3q = [quantize(g3[0], N, "w3q0")]
-        pick(1, PACK - 1, 0, HALF)
-        weave(nc.vector.tensor_copy, 0, 0)
+        pick(1, PACK - 1, 0)
+        squash(1, 0)
+        scale_round(0, 0)
         w3q.append(quantize(g3[1], N, "w3q1"))
         features(0, 0)
         for i in range(PACK):
-            squash(1, i, 0, HALF)
+            pick(0, i, 1)
 
         w4p = held([P, 2, N], I32, "w4p")
         nc.vector.tensor_copy(out=w4p[:].rearrange("p a (t m) -> p a m t", t=PACK),
@@ -344,19 +352,19 @@ def tile_list_stigma_purity_scores_kernel(
             if u == 1:
                 nc.sync.dma_start(out=rows_out[:, i, :], in_=pages[i][:])
 
-        weave(nc.vector.tensor_copy, 1, 0)
-        pick(1, 0, HALF, HALF, late)
+        scale_round(1, 0)
+        pick(1, 0, 1)
         features(1, 0)
         for i in range(1, PACK):
-            pick(1, i, HALF, HALF, late + 1024 * i)
+            pick(1, i, 1)
         scores(0, 0)
         scores(0, 1)
-        weave(nc.scalar.copy, 0, 1)
-        for i in range(PACK):
-            squash(1, i, HALF, HALF)
-        weave(nc.scalar.copy, 1, 1)
-        file_scores(0, 0)
+        squash(0, 1)
+        squash(1, 1)
+        scale_round(0, 1)
+        scale_round(1, 1)
         features(0, 1)
+        file_scores(0, 0)
         features(1, 1)
         file_scores(0, 1)
         file_scores(0, 2)

@@ -19,9 +19,21 @@ ALU = mybir.AluOpType
 P = 128
 PACK = 4
 KP = P * PACK
+PASSES = 2
 BANK = 512
 HALF = M // 2
 PER_COL = 16
+QUADRANT = 32
+ROWS = 4
+SECOND = 16
+
+SCALAR_BANKS, VECTOR_BANKS = 3, 5
+
+PLACE = PACK * KP * 4
+AT_W1 = {(0, 0): 0, (1, 0): PLACE, (0, 1): 2 * PLACE, (1, 1): 3 * PLACE}
+AT_W3 = (PLACE, 4 * PLACE)
+AT_CODES = 5 * PLACE
+AT_ROUNDED = 6 * PLACE
 
 
 def tile_list_stigma_purity_scores_kernel(
@@ -38,323 +50,296 @@ def tile_list_stigma_purity_scores_kernel(
         def held(shape, dtype, name):
             return keep.tile(shape, dtype, name=name, tag=name, align_bytes=64)
 
+        def placed(shape, dtype, name, offset):
+            return arena.tile(shape, dtype, name=name, align_bytes=64, offset=offset)
+
         tab_sc = held([P, T], U8, "tab_sc")
-        w2_sc = held([P, 2, H], U8, "w2_sc")
+        w2_sc = held([P, PASSES, H], U8, "w2_sc")
         w4_sc = held([P, N], U8, "w4_sc")
         v_sc1 = held([P, S], U8, "v_sc1")
         nc.gpsimd.memset(tab_sc[:].bitcast(I32), 0)
         nc.vector.memset(w2_sc[:].bitcast(I32), 0)
-        nc.vector.memset(v_sc1[:].bitcast(I32)[96:128, :], 0)
+        nc.vector.memset(v_sc1[:].bitcast(I32)[P - QUADRANT:P, :], 0)
         nc.vector.memset(w4_sc[:].bitcast(I32), 0)
 
-        warm_in = held([P, 1], F32, "warm_in")
-        warm_out = held([P, 1], F32, "warm_out")
-        nc.vector.memset(warm_in[:], 0.0)
-        nc.scalar.activation(out=warm_out[:], in_=warm_in[:], func=ACT.Tanh)
-
-        def load_scale_rows(queue, dst, src):
-            rows = src.rearrange("a (q r) c -> r q a c", r=4)
-            for r in range(4):
-                queue.dma_start(out=dst[:].bitcast(I32)[r:P:16, :], in_=rows[r].bitcast(I32))
-
-        raws = []
-
-        def load_rows(w, a, b, place, pieces=1):
-            raw = arena.tile([P, PACK, KP], F32, name="raw%d" % len(raws), align_bytes=64, offset=place * 8192)
-            raws.append(raw)
+        def load_weights(w, a, b, name, offset, pieces=1):
+            raw = placed([P, PACK, KP], F32, name, offset)
             src = w[a * KP:(a + 1) * KP, b * KP:(b + 1) * KP].rearrange("(p j) c -> p j c", j=PACK)
             width = KP // pieces
-            for n in range(pieces):
-                cols = slice(n * width, (n + 1) * width)
+            for piece in range(pieces):
+                cols = slice(piece * width, (piece + 1) * width)
                 nc.sync.dma_start(out=raw[:, :, cols], in_=src[:, :, cols])
             return raw
 
-        def load_vec(vec, name):
-            v = held([P, 2, PACK], F32, name)
-            nc.sync.dma_start(out=v[:], in_=vec.rearrange("(b p i) -> p b i", b=2, i=PACK))
-            return v
+        def load_row_factors(vec, name):
+            factors = held([P, PASSES, PACK], F32, name)
+            nc.sync.dma_start(out=factors[:], in_=vec.rearrange("(b p i) -> p b i", b=PASSES, i=PACK))
+            return factors
 
         def load_table(a):
-            tw = held([P, T], I32, "tab_w%d" % a)
-            nc.sync.dma_start(out=tw[:], in_=tab_words[a].rearrange("p t i -> p (t i)").bitcast(I32))
-            return tw
+            words = held([P, T], I32, "tab_w%d" % a)
+            nc.sync.dma_start(out=words[:], in_=tab_words[a].rearrange("p t i -> p (t i)").bitcast(I32))
+            return words
 
         list1 = keep.tile([P, S // PER_COL], U16, name="list1")
         nc.sync.dma_start(list1[:], offs)
         wgt_t = held([P, M], F32, "wgt_t")
         nc.sync.dma_start(out=wgt_t[:], in_=wgt)
-        sv_t = load_vec(sv, "sv_t")
-        load_scale_rows(nc.sync, tab_sc, tab_scales)
+        sv_t = load_row_factors(sv, "sv_t")
+        tab_rows = tab_scales.rearrange("a (q s) t -> s q a t", s=ROWS)
+        for s in range(ROWS):
+            nc.sync.dma_start(out=tab_sc[:].bitcast(I32)[s:P:SECOND, :], in_=tab_rows[s].bitcast(I32))
         tab_w = [load_table(0)]
-        for q in range(4):
-            nc.sync.dma_start(out=w2_sc[:].bitcast(I32)[32 * q:32 * q + 4],
-                              in_=w2_scales[:, 4 * q:4 * q + 4, :].rearrange("a r c -> r a c").bitcast(I32))
-        w2_w = held([P, 2, H // 2], I32, "w2_w")
+        for q in range(P // QUADRANT):
+            rows = w2_scales[:, ROWS * q:ROWS * (q + 1), :].rearrange("a s c -> s a c")
+            nc.sync.dma_start(out=w2_sc[:].bitcast(I32)[QUADRANT * q:QUADRANT * q + ROWS], in_=rows.bitcast(I32))
+        w2_w = held([P, PASSES, H // 2], I32, "w2_w")
         nc.sync.dma_start(out=w2_w[:], in_=w2_words.rearrange("a p c -> p a c").bitcast(I32))
         w1_raw = {}
-        w1_raw[0, 0] = load_rows(w1, 0, 0, 0)
+        w1_raw[0, 0] = load_weights(w1, 0, 0, "raw0", AT_W1[0, 0])
         tab_w.append(load_table(1))
-        ga_t = load_vec(ga, "ga_t")
-        w1_raw[1, 0] = load_rows(w1, 1, 0, 1, 2)
+        ga_t = load_row_factors(ga, "ga_t")
+        w1_raw[1, 0] = load_weights(w1, 1, 0, "raw1", AT_W1[1, 0], pieces=2)
         list2 = keep.tile([P, M // PER_COL], U16, name="list2")
         nc.sync.dma_start(list2[:], offs2)
-        gu_t = load_vec(gu, "gu_t")
-        w1_raw[0, 1] = load_rows(w1, 0, 1, 2)
-        w1_raw[1, 1] = load_rows(w1, 1, 1, 3)
-        w3_raw = [load_rows(w3, a, 0, 1 + 3 * a) for a in range(2)]
-        w4_w = held([P, 2, N], I32, "w4_w")
+        gu_t = load_row_factors(gu, "gu_t")
+        w1_raw[0, 1] = load_weights(w1, 0, 1, "raw2", AT_W1[0, 1])
+        w1_raw[1, 1] = load_weights(w1, 1, 1, "raw3", AT_W1[1, 1])
+        w3_raw = [load_weights(w3, a, 0, "raw%d" % (4 + a), AT_W3[a]) for a in range(PASSES)]
+        w4_w = held([P, PASSES, N], I32, "w4_w")
         nc.sync.dma_start(out=w4_w[:], in_=w4_words.rearrange("a p c i -> p a (c i)").bitcast(I32))
-        for q in range(4):
-            nc.sync.dma_start(out=w4_sc[:].bitcast(I32)[32 * q:32 * q + 8, :],
-                              in_=w4_scales[:, 4 * q:4 * q + 4, :].bitcast(I32))
+        for q in range(P // QUADRANT):
+            nc.sync.dma_start(out=w4_sc[:].bitcast(I32)[QUADRANT * q:QUADRANT * q + PASSES * ROWS, :],
+                              in_=w4_scales[:, ROWS * q:ROWS * (q + 1), :].bitcast(I32))
         list3 = keep.tile([P, M // PER_COL], U16, name="list3")
         nc.sync.dma_start(list3[:], offs3)
         wgo_t = held([P, M], F32, "wgo_t")
         nc.sync.dma_start(out=wgo_t[:], in_=wgo)
 
         gains = {}
-        for b in range(2):
+        for b in range(PASSES):
             for i in range(PACK):
                 gains[b, i] = held([P, M], F32, "gain%d%d" % (b, i))
                 nc.scalar.activation(out=gains[b, i][:], in_=wgt_t[:], func=ACT.Copy, scale=sv_t[:, b, i:i + 1])
 
         v_sc0 = held([P, S], U8, "v_sc0")
         nc.vector.tensor_copy(out=v_sc0[:], in_=tab_sc[:].indirect(list1[:]))
-        nc.scalar.dma_start(out=v_sc1[:].bitcast(I32)[0:112, :], in_=v_sc0[:].bitcast(I32)[16:128, :])
+        nc.scalar.dma_start(out=v_sc1[:].bitcast(I32)[0:P - SECOND, :], in_=v_sc0[:].bitcast(I32)[SECOND:P, :])
         v_sc = [v_sc0, v_sc1]
         v_w = {}
 
-        def gather_words(a, c):
-            g = held([P, BANK], U32, "v_w%d%d" % (a, c))
+        def gather_words(a):
             cols = BANK // PER_COL
-            nc.vector.tensor_copy(out=g[:], in_=tab_w[a][:].bitcast(U32).indirect(list1[:, c * cols:(c + 1) * cols]))
-            v_w[a, c] = g
+            for c in range(S // BANK):
+                v_w[a, c] = held([P, BANK], U32, "v_w%d%d" % (a, c))
+                entries = list1[:, c * cols:(c + 1) * cols]
+                nc.vector.tensor_copy(out=v_w[a, c][:], in_=tab_w[a][:].bitcast(U32).indirect(entries))
 
-        gather_words(0, 0)
-        gather_words(0, 1)
         w2p = {}
         w2p_sc = {}
 
-        def deal_w2(b):
-            if b == 0:
-                sp = held([P, 2, KP], U8, "w2p_sc0")
-                wp = held([P, 2, 2 * KP], U8, "w2p0")
-            else:
-                sp = arena.tile([P, 2, KP], U8, name="w2p_sc1", align_bytes=64, offset=6 * 8192)
-                wp = arena.tile([P, 2, 2 * KP], U8, name="w2p1", align_bytes=64, offset=6 * 8192 + 2048)
-            nc.vector.tensor_copy(out=sp[:].rearrange("p a (t m) -> p a t m", t=PACK),
-                                  in_=w2_sc[:, :, b * KP:(b + 1) * KP].rearrange("p a (m t) -> p a t m", t=PACK))
-            src = w2_w[:].bitcast(U16)[:, :, b * KP:(b + 1) * KP]
-            nc.vector.tensor_copy(out=wp[:].bitcast(U16).rearrange("p a (t m) -> p a t m", t=PACK),
-                                  in_=src.rearrange("p a (m t) -> p a t m", t=PACK))
-            w2p[b] = wp
-            w2p_sc[b] = sp
+        def deal_w2(b, scales, words):
+            cols = slice(b * KP, (b + 1) * KP)
+            nc.vector.tensor_copy(out=scales[:].rearrange("p a (i m) -> p a i m", i=PACK),
+                                  in_=w2_sc[:, :, cols].rearrange("p a (m i) -> p a i m", i=PACK))
+            nc.vector.tensor_copy(out=words[:].bitcast(U16).rearrange("p a (i m) -> p a i m", i=PACK),
+                                  in_=w2_w[:].bitcast(U16)[:, :, cols].rearrange("p a (m i) -> p a i m", i=PACK))
+            w2p_sc[b] = scales
+            w2p[b] = words
 
-        deal_w2(0)
-        gather_words(1, 0)
-        gather_words(1, 1)
+        gather_words(0)
+        deal_w2(0, held([P, PASSES, KP], U8, "w2p_sc0"), held([P, PASSES, 2 * KP], U8, "w2p0"))
+        gather_words(1)
 
-        nga = held([P, 2, PACK], F32, "nga")
-        nc.gpsimd.tensor_scalar(out=nga[:], in0=ga_t[:], scalar1=-1.0, scalar2=None, op0=ALU.mult)
+        minus_ga = held([P, PASSES, PACK], F32, "nga")
+        nc.gpsimd.tensor_scalar(out=minus_ga[:], in0=ga_t[:], scalar1=-1.0, scalar2=None, op0=ALU.mult)
 
-        def grouped_tile():
+        def rounded_tile():
             return ring.tile([P, KP * PACK], BF16, name="grouped", align_bytes=64, bufs=3)
 
-        def cast(copy, grouped, raw, half):
-            cols = slice(half * P // 2, (half + 1) * P // 2)
-            dst = grouped[:].rearrange("p (t m j) -> p m j t", t=PACK, j=PACK)
-            src = raw[:].rearrange("p j (m t) -> p m j t", t=PACK)
-            copy(out=dst[:, cols], in_=src[:, cols])
+        def round_half(copy, rounded, raw, half):
+            part = slice(half * P // 2, (half + 1) * P // 2)
+            dst = rounded[:].rearrange("p (i m j) -> p m j i", i=PACK, j=PACK)
+            src = raw[:].rearrange("p j (m i) -> p m j i", i=PACK)
+            copy(out=dst[:, part], in_=src[:, part])
 
-        def quantize(grouped, width, name, place=None):
-            if place is None:
-                codes = held([P, width], U32, name + "_w")
-            else:
-                codes = arena.tile([P, width], U32, name=name + "_w", align_bytes=64, offset=place)
-            scales = held([P, width], U8, name + "_s")
-            nc.vector.quantize_mx(out=codes[:].bitcast(FP8X4), scales=scales[:], in_=grouped[:])
+        def quantize(rounded, codes, name):
+            scales = held([P, codes.shape[1]], U8, name)
+            nc.vector.quantize_mx(out=codes[:].bitcast(FP8X4), scales=scales[:], in_=rounded[:])
             return codes, scales
 
         h = {}
+        w1q = {}
 
         def foreign(b, i):
+            name = "h%d%d" % (b, i)
             if b == 0 and i < 2:
-                ht = arena.tile([P, S], F32, name="h%d%d" % (b, i), align_bytes=64, offset=4096 * i)
+                h[b, i] = placed([P, S], F32, name, AT_W1[0, 0] + i * S * 4)
             else:
-                ht = held([P, S], F32, "h%d%d" % (b, i))
-            for c in range(2):
+                h[b, i] = held([P, S], F32, name)
+            for c in range(S // BANK):
                 cols = slice(c * BANK, (c + 1) * BANK)
-                acc = psum.tile([P, BANK], F32, name="acc_s", bufs=3)
-                for a in range(2):
+                acc = psum.tile([P, BANK], F32, name="acc_s", bufs=SCALAR_BANKS)
+                for a in range(PASSES):
                     nc.tensor.matmul_mx(
                         out=acc[:],
                         lhsT=w2p[b][:, a, 2 * P * i:2 * P * (i + 1)].bitcast(FP4X4),
                         lhsT_scale=w2p_sc[b][:, a, P * i:P * (i + 1)],
                         rhs=v_w[a, c][:].bitcast(FP8X4), rhs_scale=v_sc[a][:, cols],
-                        start=(a == 0), stop=(a == 1))
-                nc.scalar.activation(out=ht[:, cols], in_=acc[:], func=ACT.Abs)
-            h[b, i] = ht
-
-        w1q = {}
+                        start=(a == 0), stop=(a == PASSES - 1))
+                nc.scalar.activation(out=h[b, i][:, cols], in_=acc[:], func=ACT.Abs)
 
         def stigma(b, i):
-            ht = h[b, i]
-            for c in range(2):
+            for c in range(S // BANK):
                 cols = slice(c * BANK, (c + 1) * BANK)
-                acc = psum.tile([P, BANK], F32, name="acc_v", bufs=5)
-                for a in range(2):
+                acc = psum.tile([P, BANK], F32, name="acc_v", bufs=VECTOR_BANKS)
+                for a in range(PASSES):
                     codes, scales = w1q[a, b]
                     nc.tensor.matmul_mx(
                         out=acc[:],
                         lhsT=codes[:, P * i:P * (i + 1)].bitcast(FP8X4),
                         lhsT_scale=scales[:, P * i:P * (i + 1)],
                         rhs=v_w[a, c][:].bitcast(FP8X4), rhs_scale=v_sc[a][:, cols],
-                        start=(a == 0), stop=(a == 1))
-                nc.vector.scalar_tensor_tensor(out=ht[:, cols], in0=ht[:, cols], scalar=nga[:, b, i:i + 1],
-                                               in1=acc[:], op0=ALU.mult, op1=ALU.add)
+                        start=(a == 0), stop=(a == PASSES - 1))
+                nc.vector.scalar_tensor_tensor(out=h[b, i][:, cols], in0=h[b, i][:, cols],
+                                               scalar=minus_ga[:, b, i:i + 1], in1=acc[:],
+                                               op0=ALU.mult, op1=ALU.add)
 
-        late = 5 * 8192
-        zs = {}
-        for b in range(2):
-            for u in range(2):
+        picked = {}
+        for b in range(PASSES):
+            for u in range(M // HALF):
                 if b == 1 and u == 1:
-                    zs[b, u] = arena.tile([P, PACK, HALF], F32, name="late_z", align_bytes=64, offset=late)
+                    picked[b, u] = placed([P, PACK, HALF], F32, "late_z", AT_CODES)
                 else:
-                    zs[b, u] = held([P, PACK, HALF], F32, "z%d%d" % (b, u))
+                    picked[b, u] = held([P, PACK, HALF], F32, "z%d%d" % (b, u))
 
         def pick(b, i, u):
             entries = list2[:, u * HALF // PER_COL:(u + 1) * HALF // PER_COL]
-            nc.vector.tensor_tensor(out=zs[b, u][:, i, :], in0=h[b, i][:].indirect(entries),
+            nc.vector.tensor_tensor(out=picked[b, u][:, i, :], in0=h[b, i][:].indirect(entries),
                                     in1=gains[b, i][:, u * HALF:(u + 1) * HALF], op=ALU.mult)
 
         squashed = {}
-        rounded = {}
+        x_rounded = {}
         xq = {}
 
         def squash(b, u):
-            th = ring.tile([P, HALF, PACK], F32, name="th", align_bytes=64, bufs=2)
-            nc.scalar.activation(out=th[:], in_=zs[b, u][:].rearrange("p t m -> p m t"), func=ACT.Tanh)
-            squashed[b, u] = th
+            squashed[b, u] = ring.tile([P, HALF, PACK], F32, name="th", align_bytes=64, bufs=2)
+            nc.scalar.activation(out=squashed[b, u][:], in_=picked[b, u][:].rearrange("p i m -> p m i"),
+                                 func=ACT.Tanh)
 
         def scale_round(b, u):
-            xi = ring.tile([P, HALF * PACK], BF16, name="xi", align_bytes=64, bufs=2)
-            nc.vector.tensor_tensor(out=xi[:].rearrange("p (m t) -> p m t", t=PACK), in0=squashed[b, u][:],
+            x_rounded[b, u] = ring.tile([P, HALF * PACK], BF16, name="xi", align_bytes=64, bufs=2)
+            nc.vector.tensor_tensor(out=x_rounded[b, u][:].rearrange("p (m i) -> p m i", i=PACK),
+                                    in0=squashed[b, u][:],
                                     in1=gu_t[:, b, :].unsqueeze(1).to_broadcast([P, HALF, PACK]), op=ALU.mult)
-            rounded[b, u] = xi
 
-        def features(b, u):
-            xq[b, u] = quantize(rounded[b, u], HALF, "x%d%d" % (b, u))
+        def quantize_x(b, u):
+            name = "x%d%d" % (b, u)
+            xq[b, u] = quantize(x_rounded[b, u], held([P, HALF], U32, name + "_w"), name + "_s")
 
-        def cast_whole(raw, grouped):
-            for half in range(2):
-                cast(nc.scalar.copy, grouped, raw, half)
-            return grouped
-
-        g00 = cast_whole(w1_raw[0, 0], grouped_tile())
-        g10 = arena.tile([P, KP * PACK], BF16, name="g10", align_bytes=64, offset=6 * 8192)
-        cast(nc.vector.tensor_copy, g10, w1_raw[1, 0], 0)
-        w1q[0, 0] = quantize(g00, KP, "w1q00")
-        cast(nc.vector.tensor_copy, g10, w1_raw[1, 0], 1)
+        w1_00 = rounded_tile()
+        for half in range(2):
+            round_half(nc.scalar.copy, w1_00, w1_raw[0, 0], half)
+        w1_10 = placed([P, KP * PACK], BF16, "g10", AT_ROUNDED)
+        round_half(nc.vector.tensor_copy, w1_10, w1_raw[1, 0], 0)
+        w1q[0, 0] = quantize(w1_00, held([P, KP], U32, "w1q00_w"), "w1q00_s")
+        round_half(nc.vector.tensor_copy, w1_10, w1_raw[1, 0], 1)
         foreign(0, 0)
-        w1q[1, 0] = quantize(g10, KP, "w1q10")
-        deal_w2(1)
+        w1q[1, 0] = quantize(w1_10, held([P, KP], U32, "w1q10_w"), "w1q10_s")
+        deal_w2(1, placed([P, PASSES, KP], U8, "w2p_sc1", AT_ROUNDED),
+                placed([P, PASSES, 2 * KP], U8, "w2p1", AT_ROUNDED + PASSES * 2 * KP))
 
-        g1 = [grouped_tile(), grouped_tile()]
+        w1_b1 = [rounded_tile(), rounded_tile()]
         stigma(0, 0)
         foreign(0, 1)
-        cast(nc.scalar.copy, g1[0], w1_raw[0, 1], 0)
+        round_half(nc.scalar.copy, w1_b1[0], w1_raw[0, 1], 0)
         stigma(0, 1)
         foreign(0, 2)
         pick(0, 0, 0)
-        cast(nc.scalar.copy, g1[0], w1_raw[0, 1], 1)
-        cast(nc.scalar.copy, g1[1], w1_raw[1, 1], 0)
+        round_half(nc.scalar.copy, w1_b1[0], w1_raw[0, 1], 1)
+        round_half(nc.scalar.copy, w1_b1[1], w1_raw[1, 1], 0)
         stigma(0, 2)
         foreign(0, 3)
-        w1q[0, 1] = quantize(g1[0], KP, "w1q01", late)
+        w1q[0, 1] = quantize(w1_b1[0], placed([P, KP], U32, "w1q01_w", AT_CODES), "w1q01_s")
         pick(0, 1, 0)
-        cast(nc.scalar.copy, g1[1], w1_raw[1, 1], 1)
+        round_half(nc.scalar.copy, w1_b1[1], w1_raw[1, 1], 1)
         stigma(0, 3)
         foreign(1, 0)
-        w1q[1, 1] = quantize(g1[1], KP, "w1q11", late + 2048)
+        w1q[1, 1] = quantize(w1_b1[1], placed([P, KP], U32, "w1q11_w", AT_CODES + KP * 4), "w1q11_s")
         pick(0, 2, 0)
-        g3 = []
+        w3_rounded = []
         for i in range(PACK):
             stigma(1, i)
             if i + 1 < PACK:
                 foreign(1, i + 1)
             if i == 0:
-                pick(0, 3, 0)
+                pick(0, PACK - 1, 0)
             else:
                 pick(1, i - 1, 0)
             if i % 2 == 0:
-                g3.append(grouped_tile())
-            cast(nc.scalar.copy, g3[i // 2], w3_raw[i // 2], i % 2)
+                w3_rounded.append(rounded_tile())
+            round_half(nc.scalar.copy, w3_rounded[i // 2], w3_raw[i // 2], i % 2)
         squash(0, 0)
-        w3q = [quantize(g3[0], N, "w3q0")]
+        w3q = [quantize(w3_rounded[0], held([P, N], U32, "w3q0_w"), "w3q0_s")]
         pick(1, PACK - 1, 0)
         squash(1, 0)
         scale_round(0, 0)
-        w3q.append(quantize(g3[1], N, "w3q1"))
-        features(0, 0)
+        w3q.append(quantize(w3_rounded[1], held([P, N], U32, "w3q1_w"), "w3q1_s"))
+        quantize_x(0, 0)
         for i in range(PACK):
             pick(0, i, 1)
 
-        w4p = held([P, 2, N], I32, "w4p")
-        nc.vector.tensor_copy(out=w4p[:].rearrange("p a (t m) -> p a m t", t=PACK),
-                              in_=w4_w[:].rearrange("p a (m t) -> p a m t", t=PACK))
+        w4p = held([P, PASSES, N], I32, "w4p")
+        nc.vector.tensor_copy(out=w4p[:].rearrange("p a (i m) -> p a m i", i=PACK),
+                              in_=w4_w[:].rearrange("p a (m i) -> p a m i", i=PACK))
         w4p_sc = held([P, N], U8, "w4p_sc")
-        nc.vector.tensor_copy(out=w4p_sc[:].rearrange("p (t m) -> p t m", t=PACK),
-                              in_=w4_sc[:].rearrange("p (m t) -> p t m", t=PACK))
+        nc.vector.tensor_copy(out=w4p_sc[:].rearrange("p (i m) -> p i m", i=PACK),
+                              in_=w4_sc[:].rearrange("p (m i) -> p i m", i=PACK))
 
-        pages = [keep.tile([P, SLOTS], F32, name="page%d" % i, tag=tag, align_bytes=64)
-                 for i, tag in enumerate(("page0", "page1", "page2", "page3"))]
+        pages = [held([P, SLOTS], F32, "page%d" % i) for i in range(PACK)]
         for page in pages:
             nc.vector.memset(page[:], 0.0)
 
-        ys = {}
+        best = {}
 
         def scores(u, pair):
-            acc3 = psum.tile([P, BANK], F32, name="acc_s", bufs=3)
-            acc4 = psum.tile([P, BANK], F32, name="acc_v", bufs=5)
+            acc3 = psum.tile([P, BANK], F32, name="acc_s", bufs=SCALAR_BANKS)
+            acc4 = psum.tile([P, BANK], F32, name="acc_v", bufs=VECTOR_BANKS)
             for e in range(2):
-                i = 2 * pair + e
-                cols = slice(e * HALF, (e + 1) * HALF)
-                for a in range(2):
+                cols = slice(P * (2 * pair + e), P * (2 * pair + e + 1))
+                for a in range(PASSES):
                     nc.tensor.matmul_mx(
-                        out=acc3[:, cols],
-                        lhsT=w3q[a][0][:, P * i:P * (i + 1)].bitcast(FP8X4),
-                        lhsT_scale=w3q[a][1][:, P * i:P * (i + 1)],
+                        out=acc3[:, e * HALF:(e + 1) * HALF],
+                        lhsT=w3q[a][0][:, cols].bitcast(FP8X4), lhsT_scale=w3q[a][1][:, cols],
                         rhs=xq[a, u][0][:].bitcast(FP8X4), rhs_scale=xq[a, u][1][:],
-                        start=(a == 0), stop=(a == 1))
+                        start=(a == 0), stop=(a == PASSES - 1))
             for e in range(2):
-                i = 2 * pair + e
-                cols = slice(e * HALF, (e + 1) * HALF)
-                for a in range(2):
+                cols = slice(P * (2 * pair + e), P * (2 * pair + e + 1))
+                for a in range(PASSES):
                     nc.tensor.matmul_mx(
-                        out=acc4[:, cols],
-                        lhsT=w4p[:, a, P * i:P * (i + 1)].bitcast(FP8X4),
-                        lhsT_scale=w4p_sc[4 * a:P, P * i:P * (i + 1)],
+                        out=acc4[:, e * HALF:(e + 1) * HALF],
+                        lhsT=w4p[:, a, cols].bitcast(FP8X4), lhsT_scale=w4p_sc[ROWS * a:P, cols],
                         rhs=xq[a, u][0][:].bitcast(FP8X4), rhs_scale=xq[a, u][1][:],
-                        start=(a == 0), stop=(a == 1))
+                        start=(a == 0), stop=(a == PASSES - 1))
             y3 = ring.tile([P, BANK], F32, name="y3", align_bytes=64, bufs=2)
             nc.scalar.copy(out=y3[:], in_=acc3[:])
             y = ring.tile([P, BANK], F32, name="y", align_bytes=64)
             nc.vector.tensor_tensor(out=y[:], in0=acc4[:], in1=y3[:], op=ALU.max)
-            ys[u, pair] = y
+            best[u, pair] = y
 
-        rows_out = out.rearrange("(p i) s -> p i s", i=PACK)
+        out_rows = out.rearrange("(p i) s -> p i s", i=PACK)
 
         def file_scores(u, i):
-            cols = HALF // PER_COL
-            y = ys[u, i // 2][:, (i % 2) * HALF:(i % 2 + 1) * HALF]
-            nc.vector.tensor_tensor(out=pages[i][:].indirect(list3[:, u * cols:(u + 1) * cols]), in0=y,
+            entries = list3[:, u * HALF // PER_COL:(u + 1) * HALF // PER_COL]
+            y = best[u, i // 2][:, (i % 2) * HALF:(i % 2 + 1) * HALF]
+            nc.vector.tensor_tensor(out=pages[i][:].indirect(entries), in0=y,
                                     in1=wgo_t[:, u * HALF:(u + 1) * HALF], op=ALU.mult)
             if u == 1:
-                nc.sync.dma_start(out=rows_out[:, i, :], in_=pages[i][:])
+                nc.sync.dma_start(out=out_rows[:, i, :], in_=pages[i][:])
 
         scale_round(1, 0)
         pick(1, 0, 1)
-        features(1, 0)
+        quantize_x(1, 0)
         for i in range(1, PACK):
             pick(1, i, 1)
         scores(0, 0)
@@ -363,9 +348,9 @@ def tile_list_stigma_purity_scores_kernel(
         squash(1, 1)
         scale_round(0, 1)
         scale_round(1, 1)
-        features(0, 1)
+        quantize_x(0, 1)
         file_scores(0, 0)
-        features(1, 1)
+        quantize_x(1, 1)
         file_scores(0, 1)
         file_scores(0, 2)
         scores(1, 0)

from contextlib import ExitStack

import concourse.mybir as mybir

K, T, S, H, M, N, SLOTS = 1024, 2048, 1024, 1024, 512, 512, 1024
FLOPS = 2 * (2 * K * H * S) + 2 * (2 * H * N * M)

F32 = mybir.dt.float32
BF16 = mybir.dt.bfloat16
I32 = mybir.dt.int32
U32 = mybir.dt.uint32
U16 = mybir.dt.uint16
U8 = mybir.dt.uint8
FP8X4 = mybir.dt.float8_e4m3fn_x4
FP4X4 = mybir.dt.float4_e2m1fn_x4
ACT = mybir.ActivationFunctionType
ALU = mybir.AluOpType

P = 128
PACK = 4
KP = P * PACK
PASSES = 2
BANK = 512
HALF = M // 2
PER_COL = 16
QUADRANT = 32
ROWS = 4
SECOND = 16

SCALAR_BANKS, VECTOR_BANKS = 3, 5

PLACE = PACK * KP * 4
AT_W1 = {(0, 0): 0, (1, 0): PLACE, (0, 1): 2 * PLACE, (1, 1): 3 * PLACE}
AT_W3 = (PLACE, 4 * PLACE)
AT_CODES = 5 * PLACE
AT_ROUNDED = 6 * PLACE


def tile_list_stigma_purity_scores_kernel(
    tc, tab_words, tab_scales, offs, w1, w2_words, w2_scales, ga, offs2, wgt, sv, gu,
    w3, w4_words, w4_scales, offs3, wgo, out
):
    nc = tc.nc
    with ExitStack() as ctx:
        keep = ctx.enter_context(tc.tile_pool(name="keep", bufs=1))
        ring = ctx.enter_context(tc.tile_pool(name="ring", bufs=4))
        arena = ctx.enter_context(tc.tile_pool(name="arena", bufs=1))
        psum = ctx.enter_context(tc.psum_pool(name="psum", bufs=4))

        def held(shape, dtype, name):
            return keep.tile(shape, dtype, name=name, tag=name, align_bytes=64)

        def placed(shape, dtype, name, offset):
            return arena.tile(shape, dtype, name=name, align_bytes=64, offset=offset)

        tab_sc = held([P, T], U8, "tab_sc")
        w2_sc = held([P, PASSES, H], U8, "w2_sc")
        w4_sc = held([P, N], U8, "w4_sc")
        v_sc1 = held([P, S], U8, "v_sc1")
        nc.gpsimd.memset(tab_sc[:].bitcast(I32), 0)
        nc.vector.memset(w2_sc[:].bitcast(I32), 0)
        nc.vector.memset(v_sc1[:].bitcast(I32)[P - QUADRANT:P, :], 0)
        nc.vector.memset(w4_sc[:].bitcast(I32), 0)

        def load_weights(w, a, b, name, offset, pieces=1):
            raw = placed([P, PACK, KP], F32, name, offset)
            src = w[a * KP:(a + 1) * KP, b * KP:(b + 1) * KP].rearrange("(p j) c -> p j c", j=PACK)
            width = KP // pieces
            for piece in range(pieces):
                cols = slice(piece * width, (piece + 1) * width)
                nc.sync.dma_start(out=raw[:, :, cols], in_=src[:, :, cols])
            return raw

        def load_row_factors(vec, name):
            factors = held([P, PASSES, PACK], F32, name)
            nc.sync.dma_start(out=factors[:], in_=vec.rearrange("(b p i) -> p b i", b=PASSES, i=PACK))
            return factors

        def load_table(a):
            words = held([P, T], I32, "tab_w%d" % a)
            nc.sync.dma_start(out=words[:], in_=tab_words[a].rearrange("p t i -> p (t i)").bitcast(I32))
            return words

        list1 = keep.tile([P, S // PER_COL], U16, name="list1")
        nc.sync.dma_start(list1[:], offs)
        wgt_t = held([P, M], F32, "wgt_t")
        nc.sync.dma_start(out=wgt_t[:], in_=wgt)
        sv_t = load_row_factors(sv, "sv_t")
        tab_rows = tab_scales.rearrange("a (q s) t -> s q a t", s=ROWS)
        for s in range(ROWS):
            nc.sync.dma_start(out=tab_sc[:].bitcast(I32)[s:P:SECOND, :], in_=tab_rows[s].bitcast(I32))
        tab_w = [load_table(0)]
        for q in range(P // QUADRANT):
            rows = w2_scales[:, ROWS * q:ROWS * (q + 1), :].rearrange("a s c -> s a c")
            nc.sync.dma_start(out=w2_sc[:].bitcast(I32)[QUADRANT * q:QUADRANT * q + ROWS], in_=rows.bitcast(I32))
        w2_w = held([P, PASSES, H // 2], I32, "w2_w")
        nc.sync.dma_start(out=w2_w[:], in_=w2_words.rearrange("a p c -> p a c").bitcast(I32))
        w1_raw = {}
        w1_raw[0, 0] = load_weights(w1, 0, 0, "raw0", AT_W1[0, 0])
        tab_w.append(load_table(1))
        ga_t = load_row_factors(ga, "ga_t")
        w1_raw[1, 0] = load_weights(w1, 1, 0, "raw1", AT_W1[1, 0], pieces=2)
        list2 = keep.tile([P, M // PER_COL], U16, name="list2")
        nc.sync.dma_start(list2[:], offs2)
        gu_t = load_row_factors(gu, "gu_t")
        w1_raw[0, 1] = load_weights(w1, 0, 1, "raw2", AT_W1[0, 1])
        w1_raw[1, 1] = load_weights(w1, 1, 1, "raw3", AT_W1[1, 1])
        w3_raw = [load_weights(w3, a, 0, "raw%d" % (4 + a), AT_W3[a]) for a in range(PASSES)]
        w4_w = held([P, PASSES, N], I32, "w4_w")
        nc.sync.dma_start(out=w4_w[:], in_=w4_words.rearrange("a p c i -> p a (c i)").bitcast(I32))
        for q in range(P // QUADRANT):
            nc.sync.dma_start(out=w4_sc[:].bitcast(I32)[QUADRANT * q:QUADRANT * q + PASSES * ROWS, :],
                              in_=w4_scales[:, ROWS * q:ROWS * (q + 1), :].bitcast(I32))
        list3 = keep.tile([P, M // PER_COL], U16, name="list3")
        nc.sync.dma_start(list3[:], offs3)
        wgo_t = held([P, M], F32, "wgo_t")
        nc.sync.dma_start(out=wgo_t[:], in_=wgo)

        gains = {}
        for b in range(PASSES):
            for i in range(PACK):
                gains[b, i] = held([P, M], F32, "gain%d%d" % (b, i))
                nc.scalar.activation(out=gains[b, i][:], in_=wgt_t[:], func=ACT.Copy, scale=sv_t[:, b, i:i + 1])

        v_sc0 = held([P, S], U8, "v_sc0")
        nc.vector.tensor_copy(out=v_sc0[:], in_=tab_sc[:].indirect(list1[:]))
        nc.scalar.dma_start(out=v_sc1[:].bitcast(I32)[0:P - SECOND, :], in_=v_sc0[:].bitcast(I32)[SECOND:P, :])
        v_sc = [v_sc0, v_sc1]
        v_w = {}

        def gather_words(a):
            cols = BANK // PER_COL
            for c in range(S // BANK):
                v_w[a, c] = held([P, BANK], U32, "v_w%d%d" % (a, c))
                entries = list1[:, c * cols:(c + 1) * cols]
                nc.vector.tensor_copy(out=v_w[a, c][:], in_=tab_w[a][:].bitcast(U32).indirect(entries))

        w2p = {}
        w2p_sc = {}

        def deal_w2(b, scales, words):
            cols = slice(b * KP, (b + 1) * KP)
            nc.vector.tensor_copy(out=scales[:].rearrange("p a (i m) -> p a i m", i=PACK),
                                  in_=w2_sc[:, :, cols].rearrange("p a (m i) -> p a i m", i=PACK))
            nc.vector.tensor_copy(out=words[:].bitcast(U16).rearrange("p a (i m) -> p a i m", i=PACK),
                                  in_=w2_w[:].bitcast(U16)[:, :, cols].rearrange("p a (m i) -> p a i m", i=PACK))
            w2p_sc[b] = scales
            w2p[b] = words

        gather_words(0)
        deal_w2(0, held([P, PASSES, KP], U8, "w2p_sc0"), held([P, PASSES, 2 * KP], U8, "w2p0"))
        gather_words(1)

        minus_ga = held([P, PASSES, PACK], F32, "nga")
        nc.gpsimd.tensor_scalar(out=minus_ga[:], in0=ga_t[:], scalar1=-1.0, scalar2=None, op0=ALU.mult)

        def rounded_tile():
            return ring.tile([P, KP * PACK], BF16, name="grouped", align_bytes=64, bufs=3)

        def round_half(copy, rounded, raw, half):
            part = slice(half * P // 2, (half + 1) * P // 2)
            dst = rounded[:].rearrange("p (i m j) -> p m j i", i=PACK, j=PACK)
            src = raw[:].rearrange("p j (m i) -> p m j i", i=PACK)
            copy(out=dst[:, part], in_=src[:, part])

        def quantize(rounded, codes, name):
            scales = held([P, codes.shape[1]], U8, name)
            nc.vector.quantize_mx(out=codes[:].bitcast(FP8X4), scales=scales[:], in_=rounded[:])
            return codes, scales

        h = {}
        w1q = {}

        def foreign(b, i):
            name = "h%d%d" % (b, i)
            if b == 0 and i < 2:
                h[b, i] = placed([P, S], F32, name, AT_W1[0, 0] + i * S * 4)
            else:
                h[b, i] = held([P, S], F32, name)
            for c in range(S // BANK):
                cols = slice(c * BANK, (c + 1) * BANK)
                acc = psum.tile([P, BANK], F32, name="acc_s", bufs=SCALAR_BANKS)
                for a in range(PASSES):
                    nc.tensor.matmul_mx(
                        out=acc[:],
                        lhsT=w2p[b][:, a, 2 * P * i:2 * P * (i + 1)].bitcast(FP4X4),
                        lhsT_scale=w2p_sc[b][:, a, P * i:P * (i + 1)],
                        rhs=v_w[a, c][:].bitcast(FP8X4), rhs_scale=v_sc[a][:, cols],
                        start=(a == 0), stop=(a == PASSES - 1))
                nc.scalar.activation(out=h[b, i][:, cols], in_=acc[:], func=ACT.Abs)

        def stigma(b, i):
            for c in range(S // BANK):
                cols = slice(c * BANK, (c + 1) * BANK)
                acc = psum.tile([P, BANK], F32, name="acc_v", bufs=VECTOR_BANKS)
                for a in range(PASSES):
                    codes, scales = w1q[a, b]
                    nc.tensor.matmul_mx(
                        out=acc[:],
                        lhsT=codes[:, P * i:P * (i + 1)].bitcast(FP8X4),
                        lhsT_scale=scales[:, P * i:P * (i + 1)],
                        rhs=v_w[a, c][:].bitcast(FP8X4), rhs_scale=v_sc[a][:, cols],
                        start=(a == 0), stop=(a == PASSES - 1))
                nc.vector.scalar_tensor_tensor(out=h[b, i][:, cols], in0=h[b, i][:, cols],
                                               scalar=minus_ga[:, b, i:i + 1], in1=acc[:],
                                               op0=ALU.mult, op1=ALU.add)

        picked = {}
        for b in range(PASSES):
            for u in range(M // HALF):
                if b == 1 and u == 1:
                    picked[b, u] = placed([P, PACK, HALF], F32, "late_z", AT_CODES)
                else:
                    picked[b, u] = held([P, PACK, HALF], F32, "z%d%d" % (b, u))

        def pick(b, i, u):
            entries = list2[:, u * HALF // PER_COL:(u + 1) * HALF // PER_COL]
            nc.vector.tensor_tensor(out=picked[b, u][:, i, :], in0=h[b, i][:].indirect(entries),
                                    in1=gains[b, i][:, u * HALF:(u + 1) * HALF], op=ALU.mult)

        squashed = {}
        x_rounded = {}
        xq = {}

        def squash(b, u):
            squashed[b, u] = ring.tile([P, HALF, PACK], F32, name="th", align_bytes=64, bufs=2)
            nc.scalar.activation(out=squashed[b, u][:], in_=picked[b, u][:].rearrange("p i m -> p m i"),
                                 func=ACT.Tanh)

        def scale_round(b, u):
            x_rounded[b, u] = ring.tile([P, HALF * PACK], BF16, name="xi", align_bytes=64, bufs=2)
            nc.vector.tensor_tensor(out=x_rounded[b, u][:].rearrange("p (m i) -> p m i", i=PACK),
                                    in0=squashed[b, u][:],
                                    in1=gu_t[:, b, :].unsqueeze(1).to_broadcast([P, HALF, PACK]), op=ALU.mult)

        def quantize_x(b, u):
            name = "x%d%d" % (b, u)
            xq[b, u] = quantize(x_rounded[b, u], held([P, HALF], U32, name + "_w"), name + "_s")

        w1_00 = rounded_tile()
        for half in range(2):
            round_half(nc.scalar.copy, w1_00, w1_raw[0, 0], half)
        w1_10 = placed([P, KP * PACK], BF16, "g10", AT_ROUNDED)
        round_half(nc.vector.tensor_copy, w1_10, w1_raw[1, 0], 0)
        w1q[0, 0] = quantize(w1_00, held([P, KP], U32, "w1q00_w"), "w1q00_s")
        round_half(nc.vector.tensor_copy, w1_10, w1_raw[1, 0], 1)
        foreign(0, 0)
        w1q[1, 0] = quantize(w1_10, held([P, KP], U32, "w1q10_w"), "w1q10_s")
        deal_w2(1, placed([P, PASSES, KP], U8, "w2p_sc1", AT_ROUNDED),
                placed([P, PASSES, 2 * KP], U8, "w2p1", AT_ROUNDED + PASSES * 2 * KP))

        w1_b1 = [rounded_tile(), rounded_tile()]
        stigma(0, 0)
        foreign(0, 1)
        round_half(nc.scalar.copy, w1_b1[0], w1_raw[0, 1], 0)
        stigma(0, 1)
        foreign(0, 2)
        pick(0, 0, 0)
        round_half(nc.scalar.copy, w1_b1[0], w1_raw[0, 1], 1)
        round_half(nc.scalar.copy, w1_b1[1], w1_raw[1, 1], 0)
        stigma(0, 2)
        foreign(0, 3)
        w1q[0, 1] = quantize(w1_b1[0], placed([P, KP], U32, "w1q01_w", AT_CODES), "w1q01_s")
        pick(0, 1, 0)
        round_half(nc.scalar.copy, w1_b1[1], w1_raw[1, 1], 1)
        stigma(0, 3)
        foreign(1, 0)
        w1q[1, 1] = quantize(w1_b1[1], placed([P, KP], U32, "w1q11_w", AT_CODES + KP * 4), "w1q11_s")
        pick(0, 2, 0)
        w3_rounded = []
        for i in range(PACK):
            stigma(1, i)
            if i + 1 < PACK:
                foreign(1, i + 1)
            if i == 0:
                pick(0, PACK - 1, 0)
            else:
                pick(1, i - 1, 0)
            if i % 2 == 0:
                w3_rounded.append(rounded_tile())
            round_half(nc.scalar.copy, w3_rounded[i // 2], w3_raw[i // 2], i % 2)
        squash(0, 0)
        w3q = [quantize(w3_rounded[0], held([P, N], U32, "w3q0_w"), "w3q0_s")]
        pick(1, PACK - 1, 0)
        squash(1, 0)
        scale_round(0, 0)
        w3q.append(quantize(w3_rounded[1], held([P, N], U32, "w3q1_w"), "w3q1_s"))
        quantize_x(0, 0)
        for i in range(PACK):
            pick(0, i, 1)

        w4p = held([P, PASSES, N], I32, "w4p")
        nc.vector.tensor_copy(out=w4p[:].rearrange("p a (i m) -> p a m i", i=PACK),
                              in_=w4_w[:].rearrange("p a (m i) -> p a m i", i=PACK))
        w4p_sc = held([P, N], U8, "w4p_sc")
        nc.vector.tensor_copy(out=w4p_sc[:].rearrange("p (i m) -> p i m", i=PACK),
                              in_=w4_sc[:].rearrange("p (m i) -> p i m", i=PACK))

        pages = [held([P, SLOTS], F32, "page%d" % i) for i in range(PACK)]
        for page in pages:
            nc.vector.memset(page[:], 0.0)

        best = {}

        def scores(u, pair):
            acc3 = psum.tile([P, BANK], F32, name="acc_s", bufs=SCALAR_BANKS)
            acc4 = psum.tile([P, BANK], F32, name="acc_v", bufs=VECTOR_BANKS)
            for e in range(2):
                cols = slice(P * (2 * pair + e), P * (2 * pair + e + 1))
                for a in range(PASSES):
                    nc.tensor.matmul_mx(
                        out=acc3[:, e * HALF:(e + 1) * HALF],
                        lhsT=w3q[a][0][:, cols].bitcast(FP8X4), lhsT_scale=w3q[a][1][:, cols],
                        rhs=xq[a, u][0][:].bitcast(FP8X4), rhs_scale=xq[a, u][1][:],
                        start=(a == 0), stop=(a == PASSES - 1))
            for e in range(2):
                cols = slice(P * (2 * pair + e), P * (2 * pair + e + 1))
                for a in range(PASSES):
                    nc.tensor.matmul_mx(
                        out=acc4[:, e * HALF:(e + 1) * HALF],
                        lhsT=w4p[:, a, cols].bitcast(FP8X4), lhsT_scale=w4p_sc[ROWS * a:P, cols],
                        rhs=xq[a, u][0][:].bitcast(FP8X4), rhs_scale=xq[a, u][1][:],
                        start=(a == 0), stop=(a == PASSES - 1))
            y3 = ring.tile([P, BANK], F32, name="y3", align_bytes=64, bufs=2)
            nc.scalar.copy(out=y3[:], in_=acc3[:])
            y = ring.tile([P, BANK], F32, name="y", align_bytes=64)
            nc.vector.tensor_tensor(out=y[:], in0=acc4[:], in1=y3[:], op=ALU.max)
            best[u, pair] = y

        out_rows = out.rearrange("(p i) s -> p i s", i=PACK)

        def file_scores(u, i):
            entries = list3[:, u * HALF // PER_COL:(u + 1) * HALF // PER_COL]
            y = best[u, i // 2][:, (i % 2) * HALF:(i % 2 + 1) * HALF]
            nc.vector.tensor_tensor(out=pages[i][:].indirect(entries), in0=y,
                                    in1=wgo_t[:, u * HALF:(u + 1) * HALF], op=ALU.mult)
            if u == 1:
                nc.sync.dma_start(out=out_rows[:, i, :], in_=pages[i][:])

        scale_round(1, 0)
        pick(1, 0, 1)
        quantize_x(1, 0)
        for i in range(1, PACK):
            pick(1, i, 1)
        scores(0, 0)
        scores(0, 1)
        squash(0, 1)
        squash(1, 1)
        scale_round(0, 1)
        scale_round(1, 1)
        quantize_x(0, 1)
        file_scores(0, 0)
        quantize_x(1, 1)
        file_scores(0, 1)
        file_scores(0, 2)
        scores(1, 0)
        file_scores(0, 3)
        scores(1, 1)
        for i in range(PACK):
            file_scores(1, i)
